import numpy as np
import ml_dtypes


def mxq(x, axis, fmt="e4m3"):
    dtype, down = {"e4m3": (ml_dtypes.float8_e4m3fn, 7), "e5m2": (ml_dtypes.float8_e5m2, 14)}[fmt]
    v = np.moveaxis(np.asarray(x, np.float32).astype(ml_dtypes.bfloat16).astype(np.float64), axis, -1)
    blocks = v.reshape(v.shape[:-1] + (-1, 32))
    amax = np.abs(blocks).max(-1, keepdims=True)
    byte = np.maximum(np.where(amax > 0, np.frexp(amax)[1] - 1 + 127, 0) - down, 1)
    scale = np.exp2(byte - 127.0)
    codes = (blocks / scale).astype(np.float32).astype(dtype).astype(np.float64)
    return np.moveaxis((codes * scale).reshape(v.shape), -1, axis)


WIDE = False


def mx_kscale(k):
    if not WIDE:
        return np.ones(k)
    levels = np.array([10, -10, 5, -5, 0])
    if k % 512:
        return np.exp2(np.random.permutation(np.resize(levels, k // 32))).repeat(32)
    a = np.empty((k // 512, 16))
    for p in range(k // 512):
        a[p, :8] = np.random.permutation(np.resize(levels, 8))
        for g in range(8):
            far = levels[np.abs(levels - a[p, g]) >= 10]
            a[p, g + 8] = far[np.random.randint(len(far))]
    return np.exp2(a.ravel()).repeat(32)


def f64(x):
    return np.asarray(x).astype(np.float64)


def striped(idx):
    return np.tile(idx.reshape(-1, 16).T, (8, 1)).astype(np.uint16)


def unstriped(offs):
    return offs[:16].T.reshape(-1).astype(np.int64)


E2M1 = np.array([0.0, 0.5, 1.0, 1.5, 2.0, 3.0, 4.0, 6.0, -0.0, -0.5, -1.0, -1.5, -2.0, -3.0, -4.0, -6.0])


def pack_weight(w, fmt):
    k, n = w.shape
    w = f64(np.asarray(w, np.float32).astype(ml_dtypes.bfloat16)).reshape(k // 32, 32, n)
    amax = np.abs(w).max(1)
    if fmt == "e4m3":
        byte = np.frexp(amax)[1] - 1 + 127 - 7
    else:
        mant, ex = np.frexp(amax / 6.0)
        byte = np.where(mant > 0.5, ex, ex - 1) + 127
    byte = np.clip(np.where(amax > 0, byte, 1), 1, 254)
    scaled = (w * np.exp2(127.0 - byte)[:, None, :]).reshape(k, n).astype(np.float32)
    by_word = np.ascontiguousarray(scaled.reshape(k // 512, 128, 4, n).transpose(0, 1, 3, 2))
    if fmt == "e4m3":
        words = by_word.astype(ml_dtypes.float8_e4m3fn).view(np.uint8)
    else:
        c = by_word.astype(ml_dtypes.float4_e2m1fn).view(np.uint8) & 0xF
        words = (c[..., 0::2] | (c[..., 1::2] << 4)).reshape(k // 512, 128, 2 * n)
    return np.ascontiguousarray(words), np.ascontiguousarray(byte.astype(np.uint8).reshape(k // 512, 16, n))


def unpack_weight(words, scales, fmt):
    g, _, n = scales.shape
    words = np.ascontiguousarray(words).reshape(g, 128, n, -1)
    if fmt == "e4m3":
        vals = words.view(ml_dtypes.float8_e4m3fn).astype(np.float64)
    else:
        nib = np.empty((g, 128, n, 4), np.uint8)
        nib[..., 0::2] = words & 0xF
        nib[..., 1::2] = words >> 4
        vals = E2M1[nib]
    vals = vals * np.repeat(np.exp2(scales.astype(np.float64) - 127.0), 8, axis=1)[..., None]
    return vals.transpose(0, 1, 3, 2).reshape(g * 512, n)


K, T, E, C, N = 2560, 768, 6, 128, 128
K8 = 1024


def by_expert(wq, xq):
    return np.concatenate([wq[e].T @ xq[:, e * C:(e + 1) * C] for e in range(E)], axis=1)


def setup_inputs():
    n = np.random.standard_normal
    s = mx_kscale(K)[:, None]
    w = n((E, K, N)) / np.sqrt(K) / s[None]
    w8 = [pack_weight(m[:K8], "e4m3") for m in w]
    w4 = [pack_weight(m[K8:], "e2m1") for m in w]
    return {
        "xT": (n((K, T)) * s).astype(np.float32),
        "w8_words": np.stack([m[0] for m in w8]),
        "w8_scales": np.stack([m[1] for m in w8]),
        "w4_words": np.stack([m[0] for m in w4]),
        "w4_scales": np.stack([m[1] for m in w4]),
        "gate": np.tile(np.random.uniform(0.2, 1.0, E * C), (N, 1)).astype(np.float32),
        "offs": striped(np.random.permutation(T)[:E * C]),
        "dst": striped(np.random.permutation(T)[:E * C]),
    }


def reference(xT, w8_words, w8_scales, w4_words, w4_scales, gate, offs, dst):
    idx = unstriped(offs)
    w = np.stack([np.concatenate([unpack_weight(w8_words[e], w8_scales[e], "e4m3"), unpack_weight(w4_words[e], w4_scales[e], "e2m1")]) for e in range(E)])
    xq = mxq(f64(xT)[:, idx], 0, "e4m3")
    y = by_expert(w, xq)
    out = np.zeros((N, T))
    out[:, unstriped(dst)] = f64(gate) * y
    return out

@@ -1,0 +1,174 @@
+from contextlib import ExitStack
+
+import concourse.mybir as mybir
+
+K, T, E, C, N = 2560, 768, 6, 128, 128
+P = 128
+PASSES = 5
+PASSES8 = 2
+FLOPS = 2 * K * N * E * C
+
+F32 = mybir.dt.float32
+BF16 = mybir.dt.bfloat16
+I32 = mybir.dt.int32
+U32 = mybir.dt.uint32
+U16 = mybir.dt.uint16
+U8 = mybir.dt.uint8
+FP8X4 = mybir.dt.float8_e4m3fn_x4
+FP4X4 = mybir.dt.float4_e2m1fn_x4
+MULT = mybir.AluOpType.mult
+COPY = mybir.ActivationFunctionType.Copy
+
+HALVES, WHOLE = [(0, 512), (512, 768)], [(0, 768)]
+LOADS = {2: [(0, 640), (640, 768)], 3: WHOLE, 0: WHOLE, 1: WHOLE, 4: HALVES}
+COPIES = {
+    2: [(0, 256, False), (256, 512, True), (512, 640, True), (640, 672, False), (672, 768, True)],
+    3: [(0, 352, False), (352, 512, True), (512, 768, True)],
+    0: [(0, 512, False), (512, 704, False), (704, 768, True)],
+    1: [(0, 512, False), (512, 704, False), (704, 768, True)],
+    4: [(0, 416, False), (416, 512, True), (512, 704, False), (704, 768, True)],
+}
+QUANT = {a: HALVES for a in range(5)}
+QUANT[2] = [(0, 512), (512, 640), (640, 768)]
+PLANE = {2: (0, 0), 3: (0, 12), 0: (1, 4), 1: (1, 8), 4: (1, 0)}
+ORDER = [2, 3, 0, 1, 4]
+W = 1024
+PIECES = [(0, 3), (3, 6)]
+
+
+def tile_moe_two_lin_none_kernel(tc, xT, w8_words, w8_scales, w4_words, w4_scales, gate, offs, dst, out):
+    nc = tc.nc
+    with ExitStack() as ctx:
+        keep = ctx.enter_context(tc.tile_pool(name="keep", bufs=1))
+        psum = ctx.enter_context(tc.psum_pool(name="psum", bufs=1))
+
+        offs_t = keep.tile([P, T // 16], U16, name="offs_t")
+        dst_t = keep.tile([P, T // 16], U16, name="dst_t")
+        w8 = keep.tile([P, E * 2, 4 * N], U8, name="w8", align_bytes=256)
+        w4 = keep.tile([P, E * 3, 2 * N], U8, name="w4", align_bytes=256)
+        ws = keep.tile([P, E * PASSES, N], U8, name="ws", align_bytes=256)
+        ws_in = keep.tile([16, E * PASSES, N], U8, name="ws_in", align_bytes=256)
+        gate_t = keep.tile([P, E * C], F32, name="gate_t")
+        y = keep.tile([P, E * C], F32, name="y")
+        placed = keep.tile([P, T], F32, name="placed")
+        codes = [keep.tile([P, W], I32, name=f"codes{a}", align_bytes=256) for a in range(PASSES)]
+        scales = [keep.tile([P, W], U8, name=f"scales{i}", align_bytes=256) for i in range(2)]
+        gcodes = [keep.tile([P, E * C], U32, name=f"gcodes{a}", align_bytes=256) for a in range(PASSES)]
+        gscales = [keep.tile([P, E * C], U8, name=f"gscales{i}", align_bytes=256) for i in range(2)]
+        moved = keep.tile([P, E * C], U8, name="moved", align_bytes=256)
+        grouped = [keep.tile([P, T, 4], BF16, name=f"grouped{a}", align_bytes=256) for a in range(PASSES)]
+        raw = {a: [keep.tile([P, 4, hi - lo], F32, name=f"raw{a}_{lo}") for lo, hi in LOADS[a]] for a in range(PASSES)}
+        acc = [psum.tile([N, 512], F32, name=f"acc{e}") for e in range(E)]
+
+        w8_dram = w8_words.bitcast(I32).rearrange("e a p n u -> p (e a) (n u)")
+        w4_dram = w4_words.bitcast(I32).rearrange("e a p m -> p (e a) m")
+        w8s_dram = w8_scales.bitcast(I32).rearrange("e a q n -> q (e a) n")
+        w4s_dram = w4_scales.bitcast(I32).rearrange("e a q n -> q (e a) n")
+
+        def load_x(a):
+            rows = xT[512 * a : 512 * (a + 1), :].rearrange("(p t) w -> p t w", t=4)
+            for tile, (lo, hi) in zip(raw[a], LOADS[a]):
+                nc.sync.dma_start(out=tile[:], in_=rows[:, :, lo:hi])
+
+        load_x(2)
+        nc.sync.dma_start(offs_t[:], offs)
+        nc.sync.dma_start(dst_t[:], dst)
+        for a in ORDER[1:4]:
+            load_x(a)
+        nc.sync.dma_start(out=ws_in[:, 0 : 2 * E, :].bitcast(I32), in_=w8s_dram)
+        nc.sync.dma_start(out=ws_in[:, 2 * E :, :].bitcast(I32), in_=w4s_dram)
+        load_x(4)
+        nc.gpsimd.memset(ws[:].rearrange("p e n -> p (e n)").bitcast(I32), 0)
+        for quad in range(4):
+            nc.sync.dma_start(out=ws[32 * quad : 32 * quad + 4, :, :].bitcast(I32), in_=ws_in[4 * quad : 4 * quad + 4, :, :].bitcast(I32))
+        for h in range(2):
+            nc.sync.dma_start(out=w4[:, 9 * h : 9 * h + 9, :].bitcast(I32), in_=w4_dram[:, 9 * h : 9 * h + 9, :])
+            nc.sync.dma_start(out=w8[:, 6 * h : 6 * h + 6, :].bitcast(I32), in_=w8_dram[:, 6 * h : 6 * h + 6, :])
+            if h == 0:
+                nc.sync.dma_start(out=gate_t[:], in_=gate)
+
+        for i in range(2):
+            nc.gpsimd.memset(scales[i][:].bitcast(I32), 0)
+        for a in range(PASSES):
+            nc.vector.memset(codes[a][:, T:W], 0)
+        nc.gpsimd.memset(moved[:].bitcast(I32), 0)
+
+        def interleave(a):
+            for lo, hi, on_vector in COPIES[a]:
+                tile, first = [(t, l) for t, (l, h) in zip(raw[a], LOADS[a]) if l <= lo and hi <= h][0]
+                src = tile[:, :, lo - first : hi - first].rearrange("p t (c i) -> p c t i", i=4)
+                dest = grouped[a][:, lo:hi, :].rearrange("p (c i) t -> p c t i", i=4)
+                if on_vector:
+                    nc.vector.tensor_copy(dest, src)
+                else:
+                    nc.scalar.activation(dest, src, COPY)
+
+        def quantize(a):
+            i, k = PLANE[a]
+            for lo, hi in QUANT[a]:
+                nc.vector.quantize_mx(
+                    out=codes[a][:, lo:hi].bitcast(FP8X4),
+                    scales=scales[i][k:P, lo:hi],
+                    in_=grouped[a][:, lo:hi, :].rearrange("p w t -> p (w t)"),
+                )
+
+        def pick(dest, window, lo, hi):
+            cols = slice(C * lo, C * hi)
+            nc.vector.tensor_copy(dest[:, cols], window.indirect(offs_t[:, 8 * lo : 8 * hi]))
+
+        def pick_codes(a, lo=0, hi=E):
+            pick(gcodes[a], codes[a][:].bitcast(U32), lo, hi)
+
+        def pick_scales(i):
+            pick(gscales[i], scales[i][:], 0, E)
+
+        def multiply(a, e):
+            i, k = PLANE[a]
+            cols = slice(C * e, C * (e + 1))
+            if a < PASSES8:
+                lhsT, lhsT_scale = w8[:, 2 * e + a, :].bitcast(FP8X4), ws[:, 2 * e + a, :]
+            else:
+                lhsT, lhsT_scale = w4[:, 3 * e + a - 2, :].bitcast(FP4X4), ws[:, 2 * E + 3 * e + a - 2, :]
+            nc.tensor.matmul_mx(
+                out=acc[e][:, 0:C],
+                lhsT=lhsT,
+                lhsT_scale=lhsT_scale,
+                rhs=gcodes[a][:, cols].bitcast(FP8X4),
+                rhs_scale=moved[:, cols] if a == 3 else gscales[i][k:P, cols],
+                start=(a == 2),
+                stop=(a == 4),
+            )
+
+        interleave(2)
+        quantize(2)
+        pick_codes(2)
+        interleave(3)
+        quantize(3)
+        pick_codes(3)
+        pick_scales(0)
+        nc.gpsimd.dma_start(out=moved[0:112, :].bitcast(I32), in_=gscales[0][12:124, :].bitcast(I32))
+        for lo, hi in PIECES:
+            for a in (2, 3):
+                for e in range(lo, hi):
+                    multiply(a, e)
+        interleave(0)
+        quantize(0)
+        interleave(1)
+        pick_codes(0)
+        quantize(1)
+        interleave(4)
+        pick_codes(1)
+        quantize(4)
+        pick_scales(1)
+        for lo, hi in PIECES:
+            pick_codes(4, lo, hi)
+            for a in (0, 1, 4):
+                for e in range(lo, hi):
+                    multiply(a, e)
+        for lo, hi in [(0, 3), (3, 6)]:
+            for e in range(lo, hi):
+                cols = slice(C * e, C * (e + 1))
+                nc.scalar.activation(y[:, cols], acc[e][:, 0:C], COPY)
+            cols = slice(C * lo, C * hi)
+            nc.vector.tensor_tensor(placed[:].indirect(dst_t[:, 8 * lo : 8 * hi]), y[:, cols], gate_t[:, cols], MULT)
+        nc.sync.dma_start(out=out, in_=placed[:])

@@ -19,21 +19,20 @@ FP4X4 = mybir.dt.float4_e2m1fn_x4
 MULT = mybir.AluOpType.mult
 COPY = mybir.ActivationFunctionType.Copy
 
-HALVES, WHOLE = [(0, 512), (512, 768)], [(0, 768)]
-LOADS = {2: [(0, 640), (640, 768)], 3: WHOLE, 0: WHOLE, 1: WHOLE, 4: HALVES}
-COPIES = {
-    2: [(0, 256, False), (256, 512, True), (512, 640, True), (640, 672, False), (672, 768, True)],
-    3: [(0, 352, False), (352, 512, True), (512, 768, True)],
-    0: [(0, 512, False), (512, 704, False), (704, 768, True)],
-    1: [(0, 512, False), (512, 704, False), (704, 768, True)],
-    4: [(0, 416, False), (416, 512, True), (512, 704, False), (704, 768, True)],
-}
-QUANT = {a: HALVES for a in range(5)}
-QUANT[2] = [(0, 512), (512, 640), (640, 768)]
+THIRDS = [(0, 256), (256, 512), (512, 768)]
+LOADS = {a: THIRDS for a in range(5)}
+COPIES = {a: [(lo, hi, False) for lo, hi in THIRDS] for a in range(5)}
+COPIES[2] = [(0, 128, False), (128, 256, True), (256, 384, False), (384, 512, True), (512, 640, False), (640, 768, True)]
+COPIES[3] = [(0, 256, False), (256, 512, False), (512, 672, False), (672, 768, True)]
+COPIES[1] = [(0, 256, False), (256, 512, False), (512, 640, False), (640, 768, True)]
+COPIES[4] = [(0, 256, False), (256, 512, False), (512, 608, False), (608, 768, True)]
+QUANT = {a: [(0, 512), (512, 768)] for a in range(5)}
+QUANT[2] = QUANT[4] = THIRDS
 PLANE = {2: (0, 0), 3: (0, 12), 0: (1, 4), 1: (1, 8), 4: (1, 0)}
 ORDER = [2, 3, 0, 1, 4]
 W = 1024
-PIECES = [(0, 3), (3, 6)]
+GATHERS = [(0, 2), (2, 6)]
+PIECES = [(0, 2), (2, 4), (4, 6)]
 
 
 def tile_moe_two_lin_none_kernel(tc, xT, w8_words, w8_scales, w4_words, w4_scales, gate, offs, dst, out):
@@ -47,11 +46,12 @@ def tile_moe_two_lin_none_kernel(tc, xT, w8_words, w8_scales, w4_words, w4_scale
         w8 = keep.tile([P, E * 2, 4 * N], U8, name="w8", align_bytes=256)
         w4 = keep.tile([P, E * 3, 2 * N], U8, name="w4", align_bytes=256)
         ws = keep.tile([P, E * PASSES, N], U8, name="ws", align_bytes=256)
-        ws_in = keep.tile([16, E * PASSES, N], U8, name="ws_in", align_bytes=256)
+        ws_in = keep.tile([P, E * PASSES, N], U8, name="ws_in", align_bytes=256)
         gate_t = keep.tile([P, E * C], F32, name="gate_t")
         y = keep.tile([P, E * C], F32, name="y")
         placed = keep.tile([P, T], F32, name="placed")
-        codes = [keep.tile([P, W], I32, name=f"codes{a}", align_bytes=256) for a in range(PASSES)]
+        codes_all = keep.tile([P, (PASSES - 1) * T + W], I32, name="codes_all", align_bytes=256)
+        codes = {a: codes_all[:, (PASSES - 1 - j) * T : (PASSES - 1 - j) * T + W] for j, a in enumerate(ORDER)}
         scales = [keep.tile([P, W], U8, name=f"scales{i}", align_bytes=256) for i in range(2)]
         gcodes = [keep.tile([P, E * C], U32, name=f"gcodes{a}", align_bytes=256) for a in range(PASSES)]
         gscales = [keep.tile([P, E * C], U8, name=f"gscales{i}", align_bytes=256) for i in range(2)]
@@ -72,26 +72,23 @@ def tile_moe_two_lin_none_kernel(tc, xT, w8_words, w8_scales, w4_words, w4_scale
 
         load_x(2)
         nc.sync.dma_start(offs_t[:], offs)
-        nc.sync.dma_start(dst_t[:], dst)
-        for a in ORDER[1:4]:
+        nc.sync.dma_start(out=ws_in[0:P:8, 0 : 2 * E, :].bitcast(I32), in_=w8s_dram)
+        nc.sync.dma_start(out=ws_in[0:P:8, 2 * E :, :].bitcast(I32), in_=w4s_dram)
+        for a in ORDER[1:]:
             load_x(a)
-        nc.sync.dma_start(out=ws_in[:, 0 : 2 * E, :].bitcast(I32), in_=w8s_dram)
-        nc.sync.dma_start(out=ws_in[:, 2 * E :, :].bitcast(I32), in_=w4s_dram)
-        load_x(4)
-        nc.gpsimd.memset(ws[:].rearrange("p e n -> p (e n)").bitcast(I32), 0)
-        for quad in range(4):
-            nc.sync.dma_start(out=ws[32 * quad : 32 * quad + 4, :, :].bitcast(I32), in_=ws_in[4 * quad : 4 * quad + 4, :, :].bitcast(I32))
-        for h in range(2):
-            nc.sync.dma_start(out=w4[:, 9 * h : 9 * h + 9, :].bitcast(I32), in_=w4_dram[:, 9 * h : 9 * h + 9, :])
-            nc.sync.dma_start(out=w8[:, 6 * h : 6 * h + 6, :].bitcast(I32), in_=w8_dram[:, 6 * h : 6 * h + 6, :])
-            if h == 0:
-                nc.sync.dma_start(out=gate_t[:], in_=gate)
-
         for i in range(2):
-            nc.gpsimd.memset(scales[i][:].bitcast(I32), 0)
-        for a in range(PASSES):
-            nc.vector.memset(codes[a][:, T:W], 0)
-        nc.gpsimd.memset(moved[:].bitcast(I32), 0)
+            nc.vector.memset(scales[i][:].bitcast(I32), 0)
+        nc.vector.memset(codes[ORDER[0]][:, T:W], 0)
+        nc.vector.memset(moved[:].bitcast(I32), 0)
+        nc.vector.memset(ws[:].rearrange("p e n -> p (e n)").bitcast(I32), 0)
+        for quad in range(4):
+            nc.sync.dma_start(out=ws[32 * quad : 32 * quad + 4, :, :].bitcast(I32), in_=ws_in[32 * quad : 32 * quad + 32 : 8, :, :].bitcast(I32))
+        for lo, hi in PIECES:
+            nc.sync.dma_start(out=w4[:, 3 * lo : 3 * hi, :].bitcast(I32), in_=w4_dram[:, 3 * lo : 3 * hi, :])
+            nc.sync.dma_start(out=w8[:, 2 * lo : 2 * hi, :].bitcast(I32), in_=w8_dram[:, 2 * lo : 2 * hi, :])
+            if lo == 0:
+                nc.sync.dma_start(dst_t[:], dst)
+            nc.sync.dma_start(out=gate_t[:, C * lo : C * hi], in_=gate[:, C * lo : C * hi])
 
         def interleave(a):
             for lo, hi, on_vector in COPIES[a]:
@@ -117,7 +114,7 @@ def tile_moe_two_lin_none_kernel(tc, xT, w8_words, w8_scales, w4_words, w4_scale
             nc.vector.tensor_copy(dest[:, cols], window.indirect(offs_t[:, 8 * lo : 8 * hi]))
 
         def pick_codes(a, lo=0, hi=E):
-            pick(gcodes[a], codes[a][:].bitcast(U32), lo, hi)
+            pick(gcodes[a], codes[a].bitcast(U32), lo, hi)
 
         def pick_scales(i):
             pick(gscales[i], scales[i][:], 0, E)
@@ -147,10 +144,6 @@ def tile_moe_two_lin_none_kernel(tc, xT, w8_words, w8_scales, w4_words, w4_scale
         pick_codes(3)
         pick_scales(0)
         nc.gpsimd.dma_start(out=moved[0:112, :].bitcast(I32), in_=gscales[0][12:124, :].bitcast(I32))
-        for lo, hi in PIECES:
-            for a in (2, 3):
-                for e in range(lo, hi):
-                    multiply(a, e)
         interleave(0)
         quantize(0)
         interleave(1)
@@ -159,13 +152,14 @@ def tile_moe_two_lin_none_kernel(tc, xT, w8_words, w8_scales, w4_words, w4_scale
         interleave(4)
         pick_codes(1)
         quantize(4)
-        pick_scales(1)
-        for lo, hi in PIECES:
+        for lo, hi in GATHERS:
+            pick(gscales[1], scales[1][:], lo, hi)
             pick_codes(4, lo, hi)
-            for a in (0, 1, 4):
+        for lo, hi in PIECES:
+            for a in ORDER:
                 for e in range(lo, hi):
                     multiply(a, e)
-        for lo, hi in [(0, 3), (3, 6)]:
+        for lo, hi in PIECES:
             for e in range(lo, hi):
                 cols = slice(C * e, C * (e + 1))
                 nc.scalar.activation(y[:, cols], acc[e][:, 0:C], COPY)

@@ -19,15 +19,17 @@ FP4X4 = mybir.dt.float4_e2m1fn_x4
 MULT = mybir.AluOpType.mult
 COPY = mybir.ActivationFunctionType.Copy
 
-THIRDS = [(0, 256), (256, 512), (512, 768)]
-LOADS = {a: THIRDS for a in range(5)}
-COPIES = {a: [(lo, hi, False) for lo, hi in THIRDS] for a in range(5)}
-COPIES[2] = [(0, 128, False), (128, 256, True), (256, 384, False), (384, 512, True), (512, 640, False), (640, 768, True)]
-COPIES[3] = [(0, 256, False), (256, 512, False), (512, 672, False), (672, 768, True)]
-COPIES[1] = [(0, 256, False), (256, 512, False), (512, 640, False), (640, 768, True)]
-COPIES[4] = [(0, 256, False), (256, 512, False), (512, 608, False), (608, 768, True)]
-QUANT = {a: [(0, 512), (512, 768)] for a in range(5)}
-QUANT[2] = QUANT[4] = THIRDS
+HALVES, WHOLE = [(0, 512), (512, 768)], [(0, 768)]
+LOADS = {2: [(0, 640), (640, 768)], 3: WHOLE, 0: WHOLE, 1: WHOLE, 4: HALVES}
+COPIES = {
+    2: [(0, 256, False), (256, 512, True), (512, 640, True), (640, 672, False), (672, 768, True)],
+    3: [(0, 352, False), (352, 512, True), (512, 768, True)],
+    0: [(0, 512, False), (512, 704, False), (704, 768, True)],
+    1: [(0, 512, False), (512, 704, False), (704, 768, True)],
+    4: [(0, 416, False), (416, 512, True), (512, 704, False), (704, 768, True)],
+}
+QUANT = {a: HALVES for a in range(5)}
+QUANT[2] = [(0, 512), (512, 640), (640, 768)]
 PLANE = {2: (0, 0), 3: (0, 12), 0: (1, 4), 1: (1, 8), 4: (1, 0)}
 ORDER = [2, 3, 0, 1, 4]
 W = 1024

@@ -1,6 +1,7 @@
 from contextlib import ExitStack
 
 import concourse.mybir as mybir
+from concourse.masks import make_identity
 
 K, T, E, C, N = 2560, 768, 6, 128, 128
 P = 128
@@ -19,20 +20,17 @@ FP4X4 = mybir.dt.float4_e2m1fn_x4
 MULT = mybir.AluOpType.mult
 COPY = mybir.ActivationFunctionType.Copy
 
-HALVES, WHOLE = [(0, 512), (512, 768)], [(0, 768)]
-LOADS = {2: [(0, 640), (640, 768)], 3: WHOLE, 0: WHOLE, 1: WHOLE, 4: HALVES}
+LOADS = {a: [(0, 768)] for a in range(5)}
+ON_SCALAR = {2: 256, 3: 416, 0: 768, 1: 672, 4: 672}
+QUANT = {a: [(0, 512), (512, 768)] for a in range(5)}
 COPIES = {
-    2: [(0, 256, False), (256, 512, True), (512, 640, True), (640, 672, False), (672, 768, True)],
-    3: [(0, 352, False), (352, 512, True), (512, 768, True)],
-    0: [(0, 512, False), (512, 704, False), (704, 768, True)],
-    1: [(0, 512, False), (512, 704, False), (704, 768, True)],
-    4: [(0, 416, False), (416, 512, True), (512, 704, False), (704, 768, True)],
+    a: [(lo, min(hi, s), False) for lo, hi in QUANT[a] if lo < s] + [(max(lo, s), hi, True) for lo, hi in QUANT[a] if s < hi]
+    for a, s in ON_SCALAR.items()
 }
-QUANT = {a: HALVES for a in range(5)}
-QUANT[2] = [(0, 512), (512, 640), (640, 768)]
 PLANE = {2: (0, 0), 3: (0, 12), 0: (1, 4), 1: (1, 8), 4: (1, 0)}
 ORDER = [2, 3, 0, 1, 4]
 W = 1024
+GATE_PARTS = [(0, 512), (512, 768)]
 GATHERS = [(0, 2), (2, 6)]
 PIECES = [(0, 2), (2, 4), (4, 6)]
 
@@ -49,7 +47,9 @@ def tile_moe_two_lin_none_kernel(tc, xT, w8_words, w8_scales, w4_words, w4_scale
         w4 = keep.tile([P, E * 3, 2 * N], U8, name="w4", align_bytes=256)
         ws = keep.tile([P, E * PASSES, N], U8, name="ws", align_bytes=256)
         ws_in = keep.tile([P, E * PASSES, N], U8, name="ws_in", align_bytes=256)
-        gate_t = keep.tile([P, E * C], F32, name="gate_t")
+        ident = keep.tile([P, P], F32, name="ident")
+        gate_in = [keep.tile([P, (hi - lo) // P], F32, name=f"gate_in{lo}") for lo, hi in GATE_PARTS]
+        spread = [psum.tile([P, 512], F32, name=f"spread{lo}") for lo, hi in GATE_PARTS]
         y = keep.tile([P, E * C], F32, name="y")
         placed = keep.tile([P, T], F32, name="placed")
         codes_all = keep.tile([P, (PASSES - 1) * T + W], I32, name="codes_all", align_bytes=256)
@@ -59,7 +59,7 @@ def tile_moe_two_lin_none_kernel(tc, xT, w8_words, w8_scales, w4_words, w4_scale
         gscales = [keep.tile([P, E * C], U8, name=f"gscales{i}", align_bytes=256) for i in range(2)]
         moved = keep.tile([P, E * C], U8, name="moved", align_bytes=256)
         grouped = [keep.tile([P, T, 4], BF16, name=f"grouped{a}", align_bytes=256) for a in range(PASSES)]
-        raw = {a: [keep.tile([P, 4, hi - lo], F32, name=f"raw{a}_{lo}") for lo, hi in LOADS[a]] for a in range(PASSES)}
+        raw = {a: [keep.tile([P, 4, hi - lo], F32, name=f"raw{a}_{lo}", tag=f"raw{a}_{lo}") for lo, hi in LOADS[a]] for a in range(PASSES)}
         acc = [psum.tile([N, 512], F32, name=f"acc{e}") for e in range(E)]
 
         w8_dram = w8_words.bitcast(I32).rearrange("e a p n u -> p (e a) (n u)")
@@ -74,10 +74,12 @@ def tile_moe_two_lin_none_kernel(tc, xT, w8_words, w8_scales, w4_words, w4_scale
 
         load_x(2)
         nc.sync.dma_start(offs_t[:], offs)
-        nc.sync.dma_start(out=ws_in[0:P:8, 0 : 2 * E, :].bitcast(I32), in_=w8s_dram)
-        nc.sync.dma_start(out=ws_in[0:P:8, 2 * E :, :].bitcast(I32), in_=w4s_dram)
         for a in ORDER[1:]:
             load_x(a)
+        for part, (lo, hi) in zip(gate_in, GATE_PARTS):
+            nc.sync.dma_start(out=part[:], in_=gate[0, lo:hi].rearrange("(p i) -> p i", p=P))
+        nc.sync.dma_start(out=ws_in[0:P:8, 0 : 2 * E, :].bitcast(I32), in_=w8s_dram)
+        nc.sync.dma_start(out=ws_in[0:P:8, 2 * E :, :].bitcast(I32), in_=w4s_dram)
         for i in range(2):
             nc.vector.memset(scales[i][:].bitcast(I32), 0)
         nc.vector.memset(codes[ORDER[0]][:, T:W], 0)
@@ -90,7 +92,6 @@ def tile_moe_two_lin_none_kernel(tc, xT, w8_words, w8_scales, w4_words, w4_scale
             nc.sync.dma_start(out=w8[:, 2 * lo : 2 * hi, :].bitcast(I32), in_=w8_dram[:, 2 * lo : 2 * hi, :])
             if lo == 0:
                 nc.sync.dma_start(dst_t[:], dst)
-            nc.sync.dma_start(out=gate_t[:, C * lo : C * hi], in_=gate[:, C * lo : C * hi])
 
         def interleave(a):
             for lo, hi, on_vector in COPIES[a]:
@@ -154,6 +155,13 @@ def tile_moe_two_lin_none_kernel(tc, xT, w8_words, w8_scales, w4_words, w4_scale
         interleave(4)
         pick_codes(1)
         quantize(4)
+        make_identity(nc, ident[:])
+        gate_t = keep.tile([P, E * C], F32, name="gate_t", tag="raw4_0")
+        for part, bank, (lo, hi) in zip(gate_in, spread, GATE_PARTS):
+            n = (hi - lo) // P
+            for i in range(n):
+                nc.tensor.transpose(bank[:, P * i : P * (i + 1)], part[:, i : i + 1].to_broadcast([P, P]), ident[:])
+            nc.scalar.activation(gate_t[:, lo:hi].rearrange("m (p i) -> m p i", i=n), bank[:, 0 : n * P].rearrange("m (i p) -> m p i", i=n), COPY)
         for lo, hi in GATHERS:
             pick(gscales[1], scales[1][:], lo, hi)
             pick_codes(4, lo, hi)

@@ -30,6 +30,7 @@ COPIES = {
 PLANE = {2: (0, 0), 3: (0, 12), 0: (1, 4), 1: (1, 8), 4: (1, 0)}
 ORDER = [2, 3, 0, 1, 4]
 W = 1024
+RAW_BYTES = 4 * T * 4
 GATE_PARTS = [(0, 512), (512, 768)]
 GATHERS = [(0, 2), (2, 6)]
 PIECES = [(0, 2), (2, 4), (4, 6)]
@@ -39,6 +40,7 @@ def tile_moe_two_lin_none_kernel(tc, xT, w8_words, w8_scales, w4_words, w4_scale
     nc = tc.nc
     with ExitStack() as ctx:
         keep = ctx.enter_context(tc.tile_pool(name="keep", bufs=1))
+        staged = ctx.enter_context(tc.tile_pool(name="staged", bufs=1))
         psum = ctx.enter_context(tc.psum_pool(name="psum", bufs=1))
 
         offs_t = keep.tile([P, T // 16], U16, name="offs_t")
@@ -59,7 +61,8 @@ def tile_moe_two_lin_none_kernel(tc, xT, w8_words, w8_scales, w4_words, w4_scale
         gscales = [keep.tile([P, E * C], U8, name=f"gscales{i}", align_bytes=256) for i in range(2)]
         moved = keep.tile([P, E * C], U8, name="moved", align_bytes=256)
         grouped = [keep.tile([P, T, 4], BF16, name=f"grouped{a}", align_bytes=256) for a in range(PASSES)]
-        raw = {a: [keep.tile([P, 4, hi - lo], F32, name=f"raw{a}_{lo}", tag=f"raw{a}_{lo}") for lo, hi in LOADS[a]] for a in range(PASSES)}
+        raw = {a: [staged.tile([P, 4, T], F32, name=f"raw{a}", offset=RAW_BYTES * a)] for a in range(PASSES)}
+        late = {}
         acc = [psum.tile([N, 512], F32, name=f"acc{e}") for e in range(E)]
 
         w8_dram = w8_words.bitcast(I32).rearrange("e a p n u -> p (e a) (n u)")
@@ -72,12 +75,14 @@ def tile_moe_two_lin_none_kernel(tc, xT, w8_words, w8_scales, w4_words, w4_scale
             for tile, (lo, hi) in zip(raw[a], LOADS[a]):
                 nc.sync.dma_start(out=tile[:], in_=rows[:, :, lo:hi])
 
+        def load_weights(lo, hi):
+            nc.sync.dma_start(out=w4[:, 3 * lo : 3 * hi, :].bitcast(I32), in_=w4_dram[:, 3 * lo : 3 * hi, :])
+            nc.sync.dma_start(out=w8[:, 2 * lo : 2 * hi, :].bitcast(I32), in_=w8_dram[:, 2 * lo : 2 * hi, :])
+
         load_x(2)
         nc.sync.dma_start(offs_t[:], offs)
         for a in ORDER[1:]:
             load_x(a)
-        for part, (lo, hi) in zip(gate_in, GATE_PARTS):
-            nc.sync.dma_start(out=part[:], in_=gate[0, lo:hi].rearrange("(p i) -> p i", p=P))
         nc.sync.dma_start(out=ws_in[0:P:8, 0 : 2 * E, :].bitcast(I32), in_=w8s_dram)
         nc.sync.dma_start(out=ws_in[0:P:8, 2 * E :, :].bitcast(I32), in_=w4s_dram)
         for i in range(2):
@@ -85,13 +90,9 @@ def tile_moe_two_lin_none_kernel(tc, xT, w8_words, w8_scales, w4_words, w4_scale
         nc.vector.memset(codes[ORDER[0]][:, T:W], 0)
         nc.vector.memset(moved[:].bitcast(I32), 0)
         nc.vector.memset(ws[:].rearrange("p e n -> p (e n)").bitcast(I32), 0)
-        for quad in range(4):
-            nc.sync.dma_start(out=ws[32 * quad : 32 * quad + 4, :, :].bitcast(I32), in_=ws_in[32 * quad : 32 * quad + 32 : 8, :, :].bitcast(I32))
-        for lo, hi in PIECES:
-            nc.sync.dma_start(out=w4[:, 3 * lo : 3 * hi, :].bitcast(I32), in_=w4_dram[:, 3 * lo : 3 * hi, :])
-            nc.sync.dma_start(out=w8[:, 2 * lo : 2 * hi, :].bitcast(I32), in_=w8_dram[:, 2 * lo : 2 * hi, :])
-            if lo == 0:
-                nc.sync.dma_start(dst_t[:], dst)
+        nc.sync.dma_start(dst_t[:], dst)
+        for part, (lo, hi) in zip(gate_in, GATE_PARTS):
+            nc.sync.dma_start(out=part[:], in_=gate[0, lo:hi].rearrange("(p i) -> p i", p=P))
 
         def interleave(a):
             for lo, hi, on_vector in COPIES[a]:
@@ -119,6 +120,10 @@ def tile_moe_two_lin_none_kernel(tc, xT, w8_words, w8_scales, w4_words, w4_scale
         def pick_codes(a, lo=0, hi=E):
             pick(gcodes[a], codes[a].bitcast(U32), lo, hi)
 
+        def pick_late_codes(a, behind):
+            late[a] = staged.tile([P, C], U32, name=f"late{a}", offset=RAW_BYTES * behind + 4096)
+            nc.vector.tensor_copy(late[a][:], codes[a].bitcast(U32).indirect(offs_t[:, 8 * (E - 1) : 8 * E]))
+
         def pick_scales(i):
             pick(gscales[i], scales[i][:], 0, E)
 
@@ -133,30 +138,29 @@ def tile_moe_two_lin_none_kernel(tc, xT, w8_words, w8_scales, w4_words, w4_scale
                 out=acc[e][:, 0:C],
                 lhsT=lhsT,
                 lhsT_scale=lhsT_scale,
-                rhs=gcodes[a][:, cols].bitcast(FP8X4),
+                rhs=(late[a][:] if e == E - 1 and a in late else gcodes[a][:, cols]).bitcast(FP8X4),
                 rhs_scale=moved[:, cols] if a == 3 else gscales[i][k:P, cols],
                 start=(a == 2),
                 stop=(a == 4),
             )
 
-        interleave(2)
-        quantize(2)
-        pick_codes(2)
-        interleave(3)
-        quantize(3)
-        pick_codes(3)
-        pick_scales(0)
-        nc.gpsimd.dma_start(out=moved[0:112, :].bitcast(I32), in_=gscales[0][12:124, :].bitcast(I32))
-        interleave(0)
-        quantize(0)
-        interleave(1)
-        pick_codes(0)
-        quantize(1)
-        interleave(4)
-        pick_codes(1)
-        quantize(4)
+        for before, a in zip([None] + ORDER, ORDER):
+            interleave(a)
+            quantize(a)
+            if before is not None:
+                pick_late_codes(before, a)
+            if a != ORDER[-1]:
+                pick_codes(a, 0, E - 1)
+            if a == 3:
+                pick_scales(0)
+                nc.sync.dma_start(out=moved[0:112, :].bitcast(I32), in_=gscales[0][12:124, :].bitcast(I32))
+        load_weights(*PIECES[0])
+        for quad in range(4):
+            nc.sync.dma_start(out=ws[32 * quad : 32 * quad + 4, :, :].bitcast(I32), in_=ws_in[32 * quad : 32 * quad + 32 : 8, :, :].bitcast(I32))
+        for lo, hi in PIECES[1:]:
+            load_weights(lo, hi)
         make_identity(nc, ident[:])
-        gate_t = keep.tile([P, E * C], F32, name="gate_t", tag="raw4_0")
+        gate_t = staged.tile([P, E * C], F32, name="gate_t", offset=RAW_BYTES * 4)
         for part, bank, (lo, hi) in zip(gate_in, spread, GATE_PARTS):
             n = (hi - lo) // P
             for i in range(n):

@@ -21,7 +21,7 @@ MULT = mybir.AluOpType.mult
 COPY = mybir.ActivationFunctionType.Copy
 
 LOADS = {a: [(0, 768)] for a in range(5)}
-ON_SCALAR = {2: 256, 3: 416, 0: 768, 1: 672, 4: 672}
+ON_SCALAR = {2: 288, 3: 352, 0: 672, 1: 640, 4: 608}
 QUANT = {a: [(0, 512), (512, 768)] for a in range(5)}
 COPIES = {
     a: [(lo, min(hi, s), False) for lo, hi in QUANT[a] if lo < s] + [(max(lo, s), hi, True) for lo, hi in QUANT[a] if s < hi]

@@ -32,7 +32,6 @@ ORDER = [2, 3, 0, 1, 4]
 W = 1024
 RAW_BYTES = 4 * T * 4
 GATE_PARTS = [(0, 512), (512, 768)]
-GATHERS = [(0, 2), (2, 6)]
 PIECES = [(0, 2), (2, 4), (4, 6)]
 
 
@@ -127,18 +126,20 @@ def tile_moe_two_lin_none_kernel(tc, xT, w8_words, w8_scales, w4_words, w4_scale
         def pick_scales(i):
             pick(gscales[i], scales[i][:], 0, E)
 
-        def multiply(a, e):
+        def multiply(a, e, words=None):
             i, k = PLANE[a]
             cols = slice(C * e, C * (e + 1))
             if a < PASSES8:
                 lhsT, lhsT_scale = w8[:, 2 * e + a, :].bitcast(FP8X4), ws[:, 2 * e + a, :]
             else:
                 lhsT, lhsT_scale = w4[:, 3 * e + a - 2, :].bitcast(FP4X4), ws[:, 2 * E + 3 * e + a - 2, :]
+            if words is None:
+                words = late[a][:] if e == E - 1 and a in late else gcodes[a][:, cols]
             nc.tensor.matmul_mx(
                 out=acc[e][:, 0:C],
                 lhsT=lhsT,
                 lhsT_scale=lhsT_scale,
-                rhs=(late[a][:] if e == E - 1 and a in late else gcodes[a][:, cols]).bitcast(FP8X4),
+                rhs=words.bitcast(FP8X4),
                 rhs_scale=moved[:, cols] if a == 3 else gscales[i][k:P, cols],
                 start=(a == 2),
                 stop=(a == 4),
@@ -166,17 +167,28 @@ def tile_moe_two_lin_none_kernel(tc, xT, w8_words, w8_scales, w4_words, w4_scale
             for i in range(n):
                 nc.tensor.transpose(bank[:, P * i : P * (i + 1)], part[:, i : i + 1].to_broadcast([P, P]), ident[:])
             nc.scalar.activation(gate_t[:, lo:hi].rearrange("m (p i) -> m p i", i=n), bank[:, 0 : n * P].rearrange("m (i p) -> m p i", i=n), COPY)
-        for lo, hi in GATHERS:
-            pick(gscales[1], scales[1][:], lo, hi)
-            pick_codes(4, lo, hi)
+        pick(gscales[1], scales[1][:], 0, 2)
+        pick_codes(4, 0, 2)
+        pick(gscales[1], scales[1][:], 2, E)
+        middle = staged.tile([P, 2 * C], U32, name="middle", offset=RAW_BYTES * 4 + 8192)
+        nc.vector.tensor_copy(middle[:], codes[4].bitcast(U32).indirect(offs_t[:, 8 * 2 : 8 * 4]))
         for lo, hi in PIECES:
-            for a in ORDER:
+            for a in ORDER[:-1] if hi == E else ORDER:
                 for e in range(lo, hi):
-                    multiply(a, e)
-        for lo, hi in PIECES:
+                    multiply(a, e, middle[:, C * (e - 2) : C * (e - 1)] if a == 4 and lo == 2 else None)
+
+        def place(lo, hi):
             for e in range(lo, hi):
                 cols = slice(C * e, C * (e + 1))
                 nc.scalar.activation(y[:, cols], acc[e][:, 0:C], COPY)
             cols = slice(C * lo, C * hi)
             nc.vector.tensor_tensor(placed[:].indirect(dst_t[:, 8 * lo : 8 * hi]), y[:, cols], gate_t[:, cols], MULT)
+
+        place(*PIECES[0])
+        last = staged.tile([P, 2 * C], U32, name="last", offset=RAW_BYTES * 4 + 8192)
+        nc.vector.tensor_copy(last[:], codes[4].bitcast(U32).indirect(offs_t[:, 8 * 4 : 8 * E]))
+        for e in range(4, E):
+            multiply(4, e, last[:, C * (e - 4) : C * (e - 3)])
+        for lo, hi in PIECES[1:]:
+            place(lo, hi)
         nc.sync.dma_start(out=out, in_=placed[:])

@@ -21,11 +21,19 @@ MULT = mybir.AluOpType.mult
 COPY = mybir.ActivationFunctionType.Copy
 
 LOADS = {a: [(0, 768)] for a in range(5)}
-ON_SCALAR = {2: 288, 3: 352, 0: 672, 1: 640, 4: 608}
-QUANT = {a: [(0, 512), (512, 768)] for a in range(5)}
+QUANT = {
+    2: [(512, 768), (0, 256), (256, 512)],
+    3: [(512, 768), (0, 256), (256, 512)],
+    0: [(0, 512), (512, 768)],
+    1: [(0, 512), (512, 768)],
+    4: [(0, 256), (256, 512), (512, 768)],
+}
 COPIES = {
-    a: [(lo, min(hi, s), False) for lo, hi in QUANT[a] if lo < s] + [(max(lo, s), hi, True) for lo, hi in QUANT[a] if s < hi]
-    for a, s in ON_SCALAR.items()
+    2: [("scalar", 0, 256), ("scalar", 256, 320), ("vector", 512, 768), ("vector", 320, 512)],
+    3: [("scalar", 0, 256), ("scalar", 256, 384), ("vector", 512, 768), ("vector", 384, 512)],
+    0: [("scalar", 0, 512), ("scalar", 512, 672), ("vector", 672, 768)],
+    1: [("scalar", 0, 512), ("scalar", 512, 624), ("vector", 624, 768)],
+    4: [("scalar", 0, 256), ("scalar", 256, 512), ("scalar", 512, 576), ("vector", 576, 768)],
 }
 PLANE = {2: (0, 0), 3: (0, 12), 0: (1, 4), 1: (1, 8), 4: (1, 0)}
 ORDER = [2, 3, 0, 1, 4]
@@ -59,7 +67,7 @@ def tile_moe_two_lin_none_kernel(tc, xT, w8_words, w8_scales, w4_words, w4_scale
         gcodes = [keep.tile([P, E * C], U32, name=f"gcodes{a}", align_bytes=256) for a in range(PASSES)]
         gscales = [keep.tile([P, E * C], U8, name=f"gscales{i}", align_bytes=256) for i in range(2)]
         moved = keep.tile([P, E * C], U8, name="moved", align_bytes=256)
-        grouped = [keep.tile([P, T, 4], BF16, name=f"grouped{a}", align_bytes=256) for a in range(PASSES)]
+        grouped = {}
         raw = {a: [staged.tile([P, 4, T], F32, name=f"raw{a}", offset=RAW_BYTES * a)] for a in range(PASSES)}
         late = {}
         acc = [psum.tile([N, 512], F32, name=f"acc{e}") for e in range(E)]
@@ -94,14 +102,16 @@ def tile_moe_two_lin_none_kernel(tc, xT, w8_words, w8_scales, w4_words, w4_scale
             nc.sync.dma_start(out=part[:], in_=gate[0, lo:hi].rearrange("(p i) -> p i", p=P))
 
         def interleave(a):
-            for lo, hi, on_vector in COPIES[a]:
-                tile, first = [(t, l) for t, (l, h) in zip(raw[a], LOADS[a]) if l <= lo and hi <= h][0]
-                src = tile[:, :, lo - first : hi - first].rearrange("p t (c i) -> p c t i", i=4)
-                dest = grouped[a][:, lo:hi, :].rearrange("p (c i) t -> p c t i", i=4)
-                if on_vector:
-                    nc.vector.tensor_copy(dest, src)
-                else:
+            for lo, hi in QUANT[a]:
+                grouped[a, lo] = keep.tile([P, hi - lo, 4], BF16, name=f"grouped{a}_{lo}", align_bytes=256)
+            for engine, lo, hi in COPIES[a]:
+                first = max(l for l, h in QUANT[a] if l <= lo)
+                src = raw[a][0][:, :, lo:hi].rearrange("p t (c i) -> p c t i", i=4)
+                dest = grouped[a, first][:, lo - first : hi - first, :].rearrange("p (c i) t -> p c t i", i=4)
+                if engine == "scalar":
                     nc.scalar.activation(dest, src, COPY)
+                else:
+                    nc.vector.tensor_copy(dest, src)
 
         def quantize(a):
             i, k = PLANE[a]
@@ -109,7 +119,7 @@ def tile_moe_two_lin_none_kernel(tc, xT, w8_words, w8_scales, w4_words, w4_scale
                 nc.vector.quantize_mx(
                     out=codes[a][:, lo:hi].bitcast(FP8X4),
                     scales=scales[i][k:P, lo:hi],
-                    in_=grouped[a][:, lo:hi, :].rearrange("p w t -> p (w t)"),
+                    in_=grouped[a, lo][:].rearrange("p w t -> p (w t)"),
                 )
 
         def pick(dest, window, lo, hi):

@@ -20,20 +20,20 @@ FP4X4 = mybir.dt.float4_e2m1fn_x4
 MULT = mybir.AluOpType.mult
 COPY = mybir.ActivationFunctionType.Copy
 
-LOADS = {a: [(0, 768)] for a in range(5)}
+LOADS = {a: [(0, 512), (512, 768)] if a == 4 else [(0, 768)] for a in range(5)}
 QUANT = {
     2: [(512, 768), (0, 256), (256, 512)],
     3: [(512, 768), (0, 256), (256, 512)],
     0: [(0, 512), (512, 768)],
-    1: [(0, 512), (512, 768)],
+    1: [(0, 256), (256, 512), (512, 768)],
     4: [(0, 256), (256, 512), (512, 768)],
 }
 COPIES = {
     2: [("scalar", 0, 256), ("scalar", 256, 320), ("vector", 512, 768), ("vector", 320, 512)],
     3: [("scalar", 0, 256), ("scalar", 256, 384), ("vector", 512, 768), ("vector", 384, 512)],
     0: [("scalar", 0, 512), ("scalar", 512, 672), ("vector", 672, 768)],
-    1: [("scalar", 0, 512), ("scalar", 512, 624), ("vector", 624, 768)],
-    4: [("scalar", 0, 256), ("scalar", 256, 512), ("scalar", 512, 576), ("vector", 576, 768)],
+    1: [("scalar", 0, 256), ("scalar", 256, 512), ("scalar", 512, 608), ("vector", 608, 768)],
+    4: [("scalar", 0, 256), ("scalar", 256, 512), ("scalar", 512, 624), ("vector", 624, 768)],
 }
 PLANE = {2: (0, 0), 3: (0, 12), 0: (1, 4), 1: (1, 8), 4: (1, 0)}
 ORDER = [2, 3, 0, 1, 4]
@@ -68,7 +68,7 @@ def tile_moe_two_lin_none_kernel(tc, xT, w8_words, w8_scales, w4_words, w4_scale
         gscales = [keep.tile([P, E * C], U8, name=f"gscales{i}", align_bytes=256) for i in range(2)]
         moved = keep.tile([P, E * C], U8, name="moved", align_bytes=256)
         grouped = {}
-        raw = {a: [staged.tile([P, 4, T], F32, name=f"raw{a}", offset=RAW_BYTES * a)] for a in range(PASSES)}
+        raw = {a: [staged.tile([P, 4, hi - lo], F32, name=f"raw{a}_{lo}", offset=RAW_BYTES * a + 16 * lo, align_bytes=256) for lo, hi in LOADS[a]] for a in range(PASSES)}
         late = {}
         acc = [psum.tile([N, 512], F32, name=f"acc{e}") for e in range(E)]
 
@@ -106,7 +106,8 @@ def tile_moe_two_lin_none_kernel(tc, xT, w8_words, w8_scales, w4_words, w4_scale
                 grouped[a, lo] = keep.tile([P, hi - lo, 4], BF16, name=f"grouped{a}_{lo}", align_bytes=256)
             for engine, lo, hi in COPIES[a]:
                 first = max(l for l, h in QUANT[a] if l <= lo)
-                src = raw[a][0][:, :, lo:hi].rearrange("p t (c i) -> p c t i", i=4)
+                tile, start = [(t, l) for t, (l, h) in zip(raw[a], LOADS[a]) if l <= lo < h][0]
+                src = tile[:, :, lo - start : hi - start].rearrange("p t (c i) -> p c t i", i=4)
                 dest = grouped[a, first][:, lo - first : hi - first, :].rearrange("p (c i) t -> p c t i", i=4)
                 if engine == "scalar":
                     nc.scalar.activation(dest, src, COPY)
@@ -130,7 +131,7 @@ def tile_moe_two_lin_none_kernel(tc, xT, w8_words, w8_scales, w4_words, w4_scale
             pick(gcodes[a], codes[a].bitcast(U32), lo, hi)
 
         def pick_late_codes(a, behind):
-            late[a] = staged.tile([P, C], U32, name=f"late{a}", offset=RAW_BYTES * behind + 4096)
+            late[a] = staged.tile([P, C], U32, name=f"late{a}", offset=RAW_BYTES * behind + 11264, align_bytes=256)
             nc.vector.tensor_copy(late[a][:], codes[a].bitcast(U32).indirect(offs_t[:, 8 * (E - 1) : 8 * E]))
 
         def pick_scales(i):
@@ -171,7 +172,7 @@ def tile_moe_two_lin_none_kernel(tc, xT, w8_words, w8_scales, w4_words, w4_scale
         for lo, hi in PIECES[1:]:
             load_weights(lo, hi)
         make_identity(nc, ident[:])
-        gate_t = staged.tile([P, E * C], F32, name="gate_t", offset=RAW_BYTES * 4)
+        gate_t = staged.tile([P, E * C], F32, name="gate_t", offset=RAW_BYTES * 4 + 8192, align_bytes=256)
         for part, bank, (lo, hi) in zip(gate_in, spread, GATE_PARTS):
             n = (hi - lo) // P
             for i in range(n):
@@ -180,7 +181,7 @@ def tile_moe_two_lin_none_kernel(tc, xT, w8_words, w8_scales, w4_words, w4_scale
         pick(gscales[1], scales[1][:], 0, 2)
         pick_codes(4, 0, 2)
         pick(gscales[1], scales[1][:], 2, E)
-        middle = staged.tile([P, 2 * C], U32, name="middle", offset=RAW_BYTES * 4 + 8192)
+        middle = staged.tile([P, 2 * C], U32, name="middle", offset=RAW_BYTES * 2, align_bytes=256)
         nc.vector.tensor_copy(middle[:], codes[4].bitcast(U32).indirect(offs_t[:, 8 * 2 : 8 * 4]))
         for lo, hi in PIECES:
             for a in ORDER[:-1] if hi == E else ORDER:
@@ -195,7 +196,7 @@ def tile_moe_two_lin_none_kernel(tc, xT, w8_words, w8_scales, w4_words, w4_scale
             nc.vector.tensor_tensor(placed[:].indirect(dst_t[:, 8 * lo : 8 * hi]), y[:, cols], gate_t[:, cols], MULT)
 
         place(*PIECES[0])
-        last = staged.tile([P, 2 * C], U32, name="last", offset=RAW_BYTES * 4 + 8192)
+        last = staged.tile([P, 2 * C], U32, name="last", offset=RAW_BYTES * 2, align_bytes=256)
         nc.vector.tensor_copy(last[:], codes[4].bitcast(U32).indirect(offs_t[:, 8 * 4 : 8 * E]))
         for e in range(4, E):
             multiply(4, e, last[:, C * (e - 4) : C * (e - 3)])

@@ -26,21 +26,22 @@ QUANT = {
     3: [(512, 768), (0, 256), (256, 512)],
     0: [(0, 512), (512, 768)],
     1: [(0, 256), (256, 512), (512, 768)],
-    4: [(0, 256), (256, 512), (512, 768)],
+    4: [(256, 512), (0, 256), (512, 768)],
 }
 COPIES = {
     2: [("scalar", 0, 256), ("scalar", 256, 320), ("vector", 512, 768), ("vector", 320, 512)],
     3: [("scalar", 0, 256), ("scalar", 256, 384), ("vector", 512, 768), ("vector", 384, 512)],
     0: [("scalar", 0, 512), ("scalar", 512, 672), ("vector", 672, 768)],
     1: [("scalar", 0, 256), ("scalar", 256, 512), ("scalar", 512, 608), ("vector", 608, 768)],
-    4: [("scalar", 0, 256), ("scalar", 256, 512), ("scalar", 512, 624), ("vector", 624, 768)],
+    4: [("scalar", 256, 512), ("scalar", 512, 768), ("vector", 0, 256)],
 }
 PLANE = {2: (0, 0), 3: (0, 12), 0: (1, 4), 1: (1, 8), 4: (1, 0)}
 ORDER = [2, 3, 0, 1, 4]
+SUM_ORDER = [0, 2, 3, 1, 4]
 W = 1024
 RAW_BYTES = 4 * T * 4
 GATE_PARTS = [(0, 512), (512, 768)]
-PIECES = [(0, 2), (2, 4), (4, 6)]
+PIECES = [(0, 1), (1, 3), (3, 6)]
 
 
 def tile_moe_two_lin_none_kernel(tc, xT, w8_words, w8_scales, w4_words, w4_scales, gate, offs, dst, out):
@@ -48,12 +49,13 @@ def tile_moe_two_lin_none_kernel(tc, xT, w8_words, w8_scales, w4_words, w4_scale
     with ExitStack() as ctx:
         keep = ctx.enter_context(tc.tile_pool(name="keep", bufs=1))
         staged = ctx.enter_context(tc.tile_pool(name="staged", bufs=1))
+        ring = ctx.enter_context(tc.tile_pool(name="ring", bufs=1))
         psum = ctx.enter_context(tc.psum_pool(name="psum", bufs=1))
 
         offs_t = keep.tile([P, T // 16], U16, name="offs_t")
         dst_t = keep.tile([P, T // 16], U16, name="dst_t")
-        w8 = keep.tile([P, E * 2, 4 * N], U8, name="w8", align_bytes=256)
-        w4 = keep.tile([P, E * 3, 2 * N], U8, name="w4", align_bytes=256)
+        w8 = {lo: keep.tile([P, (hi - lo) * 2, 4 * N], U8, name=f"w8_{lo}", align_bytes=256) for lo, hi in PIECES}
+        w4 = {lo: keep.tile([P, (hi - lo) * 3, 2 * N], U8, name=f"w4_{lo}", align_bytes=256) for lo, hi in PIECES}
         ws = keep.tile([P, E * PASSES, N], U8, name="ws", align_bytes=256)
         ws_in = keep.tile([P, E * PASSES, N], U8, name="ws_in", align_bytes=256)
         ident = keep.tile([P, P], F32, name="ident")
@@ -64,8 +66,8 @@ def tile_moe_two_lin_none_kernel(tc, xT, w8_words, w8_scales, w4_words, w4_scale
         codes_all = keep.tile([P, (PASSES - 1) * T + W], I32, name="codes_all", align_bytes=256)
         codes = {a: codes_all[:, (PASSES - 1 - j) * T : (PASSES - 1 - j) * T + W] for j, a in enumerate(ORDER)}
         scales = [keep.tile([P, W], U8, name=f"scales{i}", align_bytes=256) for i in range(2)]
-        gcodes = [keep.tile([P, E * C], U32, name=f"gcodes{a}", align_bytes=256) for a in range(PASSES)]
-        gscales = [keep.tile([P, E * C], U8, name=f"gscales{i}", align_bytes=256) for i in range(2)]
+        gcodes = {a: keep.tile([P, E * C], U32, name=f"gcodes{a}", align_bytes=256) for a in ORDER[:-2]}
+        gscales = [keep.tile([P, E * C], U8, name=f"gscales{i}", align_bytes=256) for i in range(1)]
         moved = keep.tile([P, E * C], U8, name="moved", align_bytes=256)
         grouped = {}
         raw = {a: [staged.tile([P, 4, hi - lo], F32, name=f"raw{a}_{lo}", offset=RAW_BYTES * a + 16 * lo, align_bytes=256) for lo, hi in LOADS[a]] for a in range(PASSES)}
@@ -77,14 +79,14 @@ def tile_moe_two_lin_none_kernel(tc, xT, w8_words, w8_scales, w4_words, w4_scale
         w8s_dram = w8_scales.bitcast(I32).rearrange("e a q n -> q (e a) n")
         w4s_dram = w4_scales.bitcast(I32).rearrange("e a q n -> q (e a) n")
 
-        def load_x(a):
+        def load_x(a, part=0):
             rows = xT[512 * a : 512 * (a + 1), :].rearrange("(p t) w -> p t w", t=4)
-            for tile, (lo, hi) in zip(raw[a], LOADS[a]):
-                nc.sync.dma_start(out=tile[:], in_=rows[:, :, lo:hi])
+            lo, hi = LOADS[a][part]
+            nc.sync.dma_start(out=raw[a][part][:], in_=rows[:, :, lo:hi])
 
         def load_weights(lo, hi):
-            nc.sync.dma_start(out=w4[:, 3 * lo : 3 * hi, :].bitcast(I32), in_=w4_dram[:, 3 * lo : 3 * hi, :])
-            nc.sync.dma_start(out=w8[:, 2 * lo : 2 * hi, :].bitcast(I32), in_=w8_dram[:, 2 * lo : 2 * hi, :])
+            nc.sync.dma_start(out=w4[lo][:].bitcast(I32), in_=w4_dram[:, 3 * lo : 3 * hi, :])
+            nc.sync.dma_start(out=w8[lo][:].bitcast(I32), in_=w8_dram[:, 2 * lo : 2 * hi, :])
 
         load_x(2)
         nc.sync.dma_start(offs_t[:], offs)
@@ -92,18 +94,22 @@ def tile_moe_two_lin_none_kernel(tc, xT, w8_words, w8_scales, w4_words, w4_scale
             load_x(a)
         nc.sync.dma_start(out=ws_in[0:P:8, 0 : 2 * E, :].bitcast(I32), in_=w8s_dram)
         nc.sync.dma_start(out=ws_in[0:P:8, 2 * E :, :].bitcast(I32), in_=w4s_dram)
+        load_x(ORDER[-1], 1)
         for i in range(2):
             nc.vector.memset(scales[i][:].bitcast(I32), 0)
         nc.vector.memset(codes[ORDER[0]][:, T:W], 0)
         nc.vector.memset(moved[:].bitcast(I32), 0)
         nc.vector.memset(ws[:].rearrange("p e n -> p (e n)").bitcast(I32), 0)
-        nc.sync.dma_start(dst_t[:], dst)
         for part, (lo, hi) in zip(gate_in, GATE_PARTS):
             nc.sync.dma_start(out=part[:], in_=gate[0, lo:hi].rearrange("(p i) -> p i", p=P))
+        load_weights(*PIECES[0])
 
         def interleave(a):
             for lo, hi in QUANT[a]:
-                grouped[a, lo] = keep.tile([P, hi - lo, 4], BF16, name=f"grouped{a}_{lo}", align_bytes=256)
+                if (a, lo) == (ORDER[-1], QUANT[a][-1][0]):
+                    grouped[a, lo] = staged.tile([P, hi - lo, 4], BF16, name=f"grouped{a}_{lo}", offset=RAW_BYTES * PASSES, align_bytes=256)
+                else:
+                    grouped[a, lo] = keep.tile([P, hi - lo, 4], BF16, name=f"grouped{a}_{lo}", align_bytes=256)
             for engine, lo, hi in COPIES[a]:
                 first = max(l for l, h in QUANT[a] if l <= lo)
                 tile, start = [(t, l) for t, (l, h) in zip(raw[a], LOADS[a]) if l <= lo < h][0]
@@ -137,69 +143,72 @@ def tile_moe_two_lin_none_kernel(tc, xT, w8_words, w8_scales, w4_words, w4_scale
         def pick_scales(i):
             pick(gscales[i], scales[i][:], 0, E)
 
-        def multiply(a, e, words=None):
+        def multiply(a, e, last_scales, tail_words):
             i, k = PLANE[a]
             cols = slice(C * e, C * (e + 1))
+            first = max(lo for lo, hi in PIECES if lo <= e)
             if a < PASSES8:
-                lhsT, lhsT_scale = w8[:, 2 * e + a, :].bitcast(FP8X4), ws[:, 2 * e + a, :]
+                lhsT, lhsT_scale = w8[first][:, 2 * (e - first) + a, :].bitcast(FP8X4), ws[:, 2 * e + a, :]
             else:
-                lhsT, lhsT_scale = w4[:, 3 * e + a - 2, :].bitcast(FP4X4), ws[:, 2 * E + 3 * e + a - 2, :]
-            if words is None:
-                words = late[a][:] if e == E - 1 and a in late else gcodes[a][:, cols]
+                lhsT, lhsT_scale = w4[first][:, 3 * (e - first) + a - 2, :].bitcast(FP4X4), ws[:, 2 * E + 3 * e + a - 2, :]
+            if a in tail_words:
+                words = tail_words[a][:]
+            else:
+                words = late[a][:] if e == E - 1 else gcodes[a][:, cols]
             nc.tensor.matmul_mx(
                 out=acc[e][:, 0:C],
                 lhsT=lhsT,
                 lhsT_scale=lhsT_scale,
                 rhs=words.bitcast(FP8X4),
-                rhs_scale=moved[:, cols] if a == 3 else gscales[i][k:P, cols],
-                start=(a == 2),
+                rhs_scale=last_scales[k:P, :] if i == 1 else moved[:, cols] if a == 3 else gscales[0][k:P, cols],
+                start=(a == (SUM_ORDER if e else ORDER)[0]),
                 stop=(a == 4),
             )
+
+        def place(e):
+            cols = slice(C * e, C * (e + 1))
+            nc.vector.tensor_tensor(y[:, cols], acc[e][:, 0:C], gate_t[:, cols], MULT)
+            nc.scalar.activation(placed[:].indirect(dst_t[:, 8 * e : 8 * (e + 1)]), y[:, cols], COPY)
 
         for before, a in zip([None] + ORDER, ORDER):
             interleave(a)
             quantize(a)
-            if before is not None:
+            if before is not None and a != ORDER[-1]:
                 pick_late_codes(before, a)
-            if a != ORDER[-1]:
+            if a not in ORDER[-2:]:
                 pick_codes(a, 0, E - 1)
             if a == 3:
                 pick_scales(0)
                 nc.sync.dma_start(out=moved[0:112, :].bitcast(I32), in_=gscales[0][12:124, :].bitcast(I32))
-        load_weights(*PIECES[0])
         for quad in range(4):
             nc.sync.dma_start(out=ws[32 * quad : 32 * quad + 4, :, :].bitcast(I32), in_=ws_in[32 * quad : 32 * quad + 32 : 8, :, :].bitcast(I32))
+        nc.sync.dma_start(dst_t[:], dst)
         for lo, hi in PIECES[1:]:
             load_weights(lo, hi)
         make_identity(nc, ident[:])
-        gate_t = staged.tile([P, E * C], F32, name="gate_t", offset=RAW_BYTES * 4 + 8192, align_bytes=256)
+        gate_t = staged.tile([P, E * C], F32, name="gate_t", offset=RAW_BYTES * 4 + 9216, align_bytes=256)
         for part, bank, (lo, hi) in zip(gate_in, spread, GATE_PARTS):
             n = (hi - lo) // P
             for i in range(n):
                 nc.tensor.transpose(bank[:, P * i : P * (i + 1)], part[:, i : i + 1].to_broadcast([P, P]), ident[:])
             nc.scalar.activation(gate_t[:, lo:hi].rearrange("m (p i) -> m p i", i=n), bank[:, 0 : n * P].rearrange("m (i p) -> m p i", i=n), COPY)
-        pick(gscales[1], scales[1][:], 0, 2)
-        pick_codes(4, 0, 2)
-        pick(gscales[1], scales[1][:], 2, E)
-        middle = staged.tile([P, 2 * C], U32, name="middle", offset=RAW_BYTES * 2, align_bytes=256)
-        nc.vector.tensor_copy(middle[:], codes[4].bitcast(U32).indirect(offs_t[:, 8 * 2 : 8 * 4]))
-        for lo, hi in PIECES:
-            for a in ORDER[:-1] if hi == E else ORDER:
-                for e in range(lo, hi):
-                    multiply(a, e, middle[:, C * (e - 2) : C * (e - 1)] if a == 4 and lo == 2 else None)
 
-        def place(lo, hi):
-            for e in range(lo, hi):
-                cols = slice(C * e, C * (e + 1))
-                nc.scalar.activation(y[:, cols], acc[e][:, 0:C], COPY)
-            cols = slice(C * lo, C * hi)
-            nc.vector.tensor_tensor(placed[:].indirect(dst_t[:, 8 * lo : 8 * hi]), y[:, cols], gate_t[:, cols], MULT)
+        def pick_ahead(e):
+            at = (RAW_BYTES * PASSES if e % 2 else RAW_BYTES * 4 + 8192 - 256) + 64 * (e // 2)
+            picked = offs_t[:, 8 * e : 8 * (e + 1)]
+            words = staged.tile([P, C], U32, name=f"fourth{e}", offset=at, align_bytes=64)
+            planes = staged.tile([P, C], U8, name=f"planes{e}", offset=at + 4 * C, align_bytes=64)
+            nc.vector.tensor_copy(planes[:], scales[1][:].indirect(picked))
+            nc.vector.tensor_copy(words[:], codes[1].bitcast(U32).indirect(picked))
+            return words, planes
 
-        place(*PIECES[0])
-        last = staged.tile([P, 2 * C], U32, name="last", offset=RAW_BYTES * 2, align_bytes=256)
-        nc.vector.tensor_copy(last[:], codes[4].bitcast(U32).indirect(offs_t[:, 8 * 4 : 8 * E]))
-        for e in range(4, E):
-            multiply(4, e, last[:, C * (e - 4) : C * (e - 3)])
-        for lo, hi in PIECES[1:]:
-            place(lo, hi)
+        fourth, planes = pick_ahead(0)
+        for e in range(E):
+            last_words = ring.tile([P, C], U32, name="last_words", align_bytes=256)
+            nc.vector.tensor_copy(last_words[:], codes[4].bitcast(U32).indirect(offs_t[:, 8 * e : 8 * (e + 1)]))
+            for a in SUM_ORDER if e else ORDER:
+                multiply(a, e, planes, {1: fourth, 4: last_words})
+            if e + 1 < E:
+                fourth, planes = pick_ahead(e + 1)
+            place(e)
         nc.sync.dma_start(out=out, in_=placed[:])

@@ -41,7 +41,6 @@ SUM_ORDER = [0, 2, 3, 1, 4]
 W = 1024
 RAW_BYTES = 4 * T * 4
 GATE_PARTS = [(0, 512), (512, 768)]
-PIECES = [(0, 1), (1, 3), (3, 6)]
 
 
 def tile_moe_two_lin_none_kernel(tc, xT, w8_words, w8_scales, w4_words, w4_scales, gate, offs, dst, out):
@@ -54,12 +53,12 @@ def tile_moe_two_lin_none_kernel(tc, xT, w8_words, w8_scales, w4_words, w4_scale
 
         offs_t = keep.tile([P, T // 16], U16, name="offs_t")
         dst_t = keep.tile([P, T // 16], U16, name="dst_t")
-        w8 = {lo: keep.tile([P, (hi - lo) * 2, 4 * N], U8, name=f"w8_{lo}", align_bytes=256) for lo, hi in PIECES}
-        w4 = {lo: keep.tile([P, (hi - lo) * 3, 2 * N], U8, name=f"w4_{lo}", align_bytes=256) for lo, hi in PIECES}
+        w8 = [keep.tile([P, 2, 4 * N], U8, name=f"w8_{e}", align_bytes=256) for e in range(E)]
+        w4 = [keep.tile([P, 3, 2 * N], U8, name=f"w4_{e}", align_bytes=256) for e in range(E)]
+        gate_in = [keep.tile([P, (hi - lo) // P], F32, name=f"gate_in{lo}") for lo, hi in GATE_PARTS]
         ws = keep.tile([P, E * PASSES, N], U8, name="ws", align_bytes=256)
         ws_in = keep.tile([P, E * PASSES, N], U8, name="ws_in", align_bytes=256)
         ident = keep.tile([P, P], F32, name="ident")
-        gate_in = [keep.tile([P, (hi - lo) // P], F32, name=f"gate_in{lo}") for lo, hi in GATE_PARTS]
         spread = [psum.tile([P, 512], F32, name=f"spread{lo}") for lo, hi in GATE_PARTS]
         y = keep.tile([P, E * C], F32, name="y")
         placed = keep.tile([P, T], F32, name="placed")
@@ -84,9 +83,9 @@ def tile_moe_two_lin_none_kernel(tc, xT, w8_words, w8_scales, w4_words, w4_scale
             lo, hi = LOADS[a][part]
             nc.sync.dma_start(out=raw[a][part][:], in_=rows[:, :, lo:hi])
 
-        def load_weights(lo, hi):
-            nc.sync.dma_start(out=w4[lo][:].bitcast(I32), in_=w4_dram[:, 3 * lo : 3 * hi, :])
-            nc.sync.dma_start(out=w8[lo][:].bitcast(I32), in_=w8_dram[:, 2 * lo : 2 * hi, :])
+        def load_weights(e):
+            nc.sync.dma_start(out=w4[e][:].bitcast(I32), in_=w4_dram[:, 3 * e : 3 * (e + 1), :])
+            nc.sync.dma_start(out=w8[e][:].bitcast(I32), in_=w8_dram[:, 2 * e : 2 * (e + 1), :])
 
         load_x(2)
         nc.sync.dma_start(offs_t[:], offs)
@@ -94,15 +93,16 @@ def tile_moe_two_lin_none_kernel(tc, xT, w8_words, w8_scales, w4_words, w4_scale
             load_x(a)
         nc.sync.dma_start(out=ws_in[0:P:8, 0 : 2 * E, :].bitcast(I32), in_=w8s_dram)
         nc.sync.dma_start(out=ws_in[0:P:8, 2 * E :, :].bitcast(I32), in_=w4s_dram)
+        nc.sync.dma_start(dst_t[:], dst)
+        for part, (lo, hi) in zip(gate_in, GATE_PARTS):
+            nc.sync.dma_start(out=part[:], in_=gate[0, lo:hi].rearrange("(p i) -> p i", p=P))
         load_x(ORDER[-1], 1)
         for i in range(2):
             nc.vector.memset(scales[i][:].bitcast(I32), 0)
         nc.vector.memset(codes[ORDER[0]][:, T:W], 0)
         nc.vector.memset(moved[:].bitcast(I32), 0)
         nc.vector.memset(ws[:].rearrange("p e n -> p (e n)").bitcast(I32), 0)
-        for part, (lo, hi) in zip(gate_in, GATE_PARTS):
-            nc.sync.dma_start(out=part[:], in_=gate[0, lo:hi].rearrange("(p i) -> p i", p=P))
-        load_weights(*PIECES[0])
+        load_weights(0)
 
         def interleave(a):
             for lo, hi in QUANT[a]:
@@ -146,11 +146,10 @@ def tile_moe_two_lin_none_kernel(tc, xT, w8_words, w8_scales, w4_words, w4_scale
         def multiply(a, e, last_scales, tail_words):
             i, k = PLANE[a]
             cols = slice(C * e, C * (e + 1))
-            first = max(lo for lo, hi in PIECES if lo <= e)
             if a < PASSES8:
-                lhsT, lhsT_scale = w8[first][:, 2 * (e - first) + a, :].bitcast(FP8X4), ws[:, 2 * e + a, :]
+                lhsT, lhsT_scale = w8[e][:, a, :].bitcast(FP8X4), ws[:, 2 * e + a, :]
             else:
-                lhsT, lhsT_scale = w4[first][:, 3 * (e - first) + a - 2, :].bitcast(FP4X4), ws[:, 2 * E + 3 * e + a - 2, :]
+                lhsT, lhsT_scale = w4[e][:, a - 2, :].bitcast(FP4X4), ws[:, 2 * E + 3 * e + a - 2, :]
             if a in tail_words:
                 words = tail_words[a][:]
             else:
@@ -182,9 +181,8 @@ def tile_moe_two_lin_none_kernel(tc, xT, w8_words, w8_scales, w4_words, w4_scale
                 nc.sync.dma_start(out=moved[0:112, :].bitcast(I32), in_=gscales[0][12:124, :].bitcast(I32))
         for quad in range(4):
             nc.sync.dma_start(out=ws[32 * quad : 32 * quad + 4, :, :].bitcast(I32), in_=ws_in[32 * quad : 32 * quad + 32 : 8, :, :].bitcast(I32))
-        nc.sync.dma_start(dst_t[:], dst)
-        for lo, hi in PIECES[1:]:
-            load_weights(lo, hi)
+        for e in range(1, E):
+            load_weights(e)
         make_identity(nc, ident[:])
         gate_t = staged.tile([P, E * C], F32, name="gate_t", offset=RAW_BYTES * 4 + 9216, align_bytes=256)
         for part, bank, (lo, hi) in zip(gate_in, spread, GATE_PARTS):

@@ -38,6 +38,7 @@ COPIES = {
 PLANE = {2: (0, 0), 3: (0, 12), 0: (1, 4), 1: (1, 8), 4: (1, 0)}
 ORDER = [2, 3, 0, 1, 4]
 SUM_ORDER = [0, 2, 3, 1, 4]
+LAST_AT = [256, 0, 512, 0, 512, 512]
 W = 1024
 RAW_BYTES = 4 * T * 4
 GATE_PARTS = [(0, 512), (512, 768)]
@@ -48,7 +49,6 @@ def tile_moe_two_lin_none_kernel(tc, xT, w8_words, w8_scales, w4_words, w4_scale
     with ExitStack() as ctx:
         keep = ctx.enter_context(tc.tile_pool(name="keep", bufs=1))
         staged = ctx.enter_context(tc.tile_pool(name="staged", bufs=1))
-        ring = ctx.enter_context(tc.tile_pool(name="ring", bufs=1))
         psum = ctx.enter_context(tc.psum_pool(name="psum", bufs=1))
 
         offs_t = keep.tile([P, T // 16], U16, name="offs_t")
@@ -200,13 +200,21 @@ def tile_moe_two_lin_none_kernel(tc, xT, w8_words, w8_scales, w4_words, w4_scale
             nc.vector.tensor_copy(words[:], codes[1].bitcast(U32).indirect(picked))
             return words, planes
 
-        fourth, planes = pick_ahead(0)
-        for e in range(E):
-            last_words = ring.tile([P, C], U32, name="last_words", align_bytes=256)
+        def finish(e, fourth, planes):
+            last_words = staged.tile([P, C], U32, name=f"last{e}", offset=RAW_BYTES * PASSES + 2048 + LAST_AT[e], align_bytes=256)
             nc.vector.tensor_copy(last_words[:], codes[4].bitcast(U32).indirect(offs_t[:, 8 * e : 8 * (e + 1)]))
             for a in SUM_ORDER if e else ORDER:
                 multiply(a, e, planes, {1: fourth, 4: last_words})
-            if e + 1 < E:
-                fourth, planes = pick_ahead(e + 1)
-            place(e)
+
+        finish(0, *pick_ahead(0))
+        ahead = pick_ahead(1)
+        place(0)
+        finish(1, *ahead)
+        for e in range(2, E - 1):
+            finish(e, *pick_ahead(e))
+            place(e - 1)
+        ahead = pick_ahead(E - 1)
+        place(E - 2)
+        finish(E - 1, *ahead)
+        place(E - 1)
         nc.sync.dma_start(out=out, in_=placed[:])

@@ -7,6 +7,7 @@ K, T, E, C, N = 2560, 768, 6, 128, 128
 P = 128
 PASSES = 5
 PASSES8 = 2
+PASSES4 = PASSES - PASSES8
 FLOPS = 2 * K * N * E * C
 
 F32 = mybir.dt.float32
@@ -20,28 +21,32 @@ FP4X4 = mybir.dt.float4_e2m1fn_x4
 MULT = mybir.AluOpType.mult
 COPY = mybir.ActivationFunctionType.Copy
 
-LOADS = {a: [(0, 512), (512, 768)] if a == 4 else [(0, 768)] for a in range(5)}
-QUANT = {
-    2: [(512, 768), (0, 256), (256, 512)],
-    3: [(512, 768), (0, 256), (256, 512)],
-    0: [(0, 512), (512, 768)],
-    1: [(0, 256), (256, 512), (512, 768)],
-    4: [(256, 512), (0, 256), (512, 768)],
-}
-COPIES = {
-    2: [("scalar", 0, 256), ("scalar", 256, 320), ("vector", 512, 768), ("vector", 320, 512)],
-    3: [("scalar", 0, 256), ("scalar", 256, 384), ("vector", 512, 768), ("vector", 384, 512)],
-    0: [("scalar", 0, 512), ("scalar", 512, 672), ("vector", 672, 768)],
-    1: [("scalar", 0, 256), ("scalar", 256, 512), ("scalar", 512, 608), ("vector", 608, 768)],
-    4: [("scalar", 256, 512), ("scalar", 512, 768), ("vector", 0, 256)],
-}
-PLANE = {2: (0, 0), 3: (0, 12), 0: (1, 4), 1: (1, 8), 4: (1, 0)}
 ORDER = [2, 3, 0, 1, 4]
+FOURTH, LAST = ORDER[-2:]
+MOVED_PASS = 3
+PLANE = {2: (0, 0), 3: (0, 12), 0: (1, 4), 1: (1, 8), 4: (1, 0)}
 SUM_ORDER = [0, 2, 3, 1, 4]
-LAST_AT = [256, 0, 512, 0, 512, 512]
+LOADS = {a: [(0, 512), (512, T)] if a == LAST else [(0, T)] for a in range(PASSES)}
+CHUNKS = {
+    2: [(512, T), (0, 256), (256, 512)],
+    3: [(512, T), (0, 256), (256, 512)],
+    0: [(0, 512), (512, T)],
+    1: [(0, 256), (256, 512), (512, T)],
+    4: [(256, 512), (0, 256), (512, T)],
+}
+ON_SCALAR = {2: (0, 320), 3: (0, 384), 0: (0, 672), 1: (0, 608), 4: (256, T)}
 W = 1024
+LIST = C // 16
+GATE_PARTS = [(0, 512), (512, T)]
+
 RAW_BYTES = 4 * T * 4
-GATE_PARTS = [(0, 512), (512, 768)]
+WORDS_BYTES = 4 * C
+LATE_AT = RAW_BYTES - 2 * WORDS_BYTES
+SEAM = RAW_BYTES * LAST + 16 * LOADS[LAST][1][0]
+GATE_AT = SEAM + 2 * WORDS_BYTES
+CHUNK_AT = RAW_BYTES * PASSES
+LAST_AT = CHUNK_AT + 8 * 256
+LAST_HALVES = [1, 0, 2, 0, 2, 2]
 
 
 def tile_moe_two_lin_none_kernel(tc, xT, w8_words, w8_scales, w4_words, w4_scales, gate, offs, dst, out):
@@ -53,8 +58,8 @@ def tile_moe_two_lin_none_kernel(tc, xT, w8_words, w8_scales, w4_words, w4_scale
 
         offs_t = keep.tile([P, T // 16], U16, name="offs_t")
         dst_t = keep.tile([P, T // 16], U16, name="dst_t")
-        w8 = [keep.tile([P, 2, 4 * N], U8, name=f"w8_{e}", align_bytes=256) for e in range(E)]
-        w4 = [keep.tile([P, 3, 2 * N], U8, name=f"w4_{e}", align_bytes=256) for e in range(E)]
+        w8 = [keep.tile([P, PASSES8, 4 * N], U8, name=f"w8_{e}", align_bytes=256) for e in range(E)]
+        w4 = [keep.tile([P, PASSES4, 2 * N], U8, name=f"w4_{e}", align_bytes=256) for e in range(E)]
         gate_in = [keep.tile([P, (hi - lo) // P], F32, name=f"gate_in{lo}") for lo, hi in GATE_PARTS]
         ws = keep.tile([P, E * PASSES, N], U8, name="ws", align_bytes=256)
         ws_in = keep.tile([P, E * PASSES, N], U8, name="ws_in", align_bytes=256)
@@ -66,7 +71,7 @@ def tile_moe_two_lin_none_kernel(tc, xT, w8_words, w8_scales, w4_words, w4_scale
         codes = {a: codes_all[:, (PASSES - 1 - j) * T : (PASSES - 1 - j) * T + W] for j, a in enumerate(ORDER)}
         scales = [keep.tile([P, W], U8, name=f"scales{i}", align_bytes=256) for i in range(2)]
         gcodes = {a: keep.tile([P, E * C], U32, name=f"gcodes{a}", align_bytes=256) for a in ORDER[:-2]}
-        gscales = [keep.tile([P, E * C], U8, name=f"gscales{i}", align_bytes=256) for i in range(1)]
+        gscales = keep.tile([P, E * C], U8, name="gscales0", align_bytes=256)
         moved = keep.tile([P, E * C], U8, name="moved", align_bytes=256)
         grouped = {}
         raw = {a: [staged.tile([P, 4, hi - lo], F32, name=f"raw{a}_{lo}", offset=RAW_BYTES * a + 16 * lo, align_bytes=256) for lo, hi in LOADS[a]] for a in range(PASSES)}
@@ -78,142 +83,142 @@ def tile_moe_two_lin_none_kernel(tc, xT, w8_words, w8_scales, w4_words, w4_scale
         w8s_dram = w8_scales.bitcast(I32).rearrange("e a q n -> q (e a) n")
         w4s_dram = w4_scales.bitcast(I32).rearrange("e a q n -> q (e a) n")
 
-        def load_x(a, part=0):
+        def load_x(a, part):
             rows = xT[512 * a : 512 * (a + 1), :].rearrange("(p t) w -> p t w", t=4)
             lo, hi = LOADS[a][part]
             nc.sync.dma_start(out=raw[a][part][:], in_=rows[:, :, lo:hi])
 
         def load_weights(e):
-            nc.sync.dma_start(out=w4[e][:].bitcast(I32), in_=w4_dram[:, 3 * e : 3 * (e + 1), :])
-            nc.sync.dma_start(out=w8[e][:].bitcast(I32), in_=w8_dram[:, 2 * e : 2 * (e + 1), :])
+            nc.sync.dma_start(out=w4[e][:].bitcast(I32), in_=w4_dram[:, PASSES4 * e : PASSES4 * (e + 1), :])
+            nc.sync.dma_start(out=w8[e][:].bitcast(I32), in_=w8_dram[:, PASSES8 * e : PASSES8 * (e + 1), :])
 
-        load_x(2)
+        load_x(ORDER[0], 0)
         nc.sync.dma_start(offs_t[:], offs)
-        for a in ORDER[1:]:
-            load_x(a)
-        nc.sync.dma_start(out=ws_in[0:P:8, 0 : 2 * E, :].bitcast(I32), in_=w8s_dram)
-        nc.sync.dma_start(out=ws_in[0:P:8, 2 * E :, :].bitcast(I32), in_=w4s_dram)
-        nc.sync.dma_start(dst_t[:], dst)
+        for a in ORDER[1:-1]:
+            load_x(a, 0)
+        nc.sync.dma_start(out=ws_in[0:P:8, 0 : PASSES8 * E, :].bitcast(I32), in_=w8s_dram)
+        nc.sync.dma_start(out=ws_in[0:P:8, PASSES8 * E :, :].bitcast(I32), in_=w4s_dram)
+        load_x(LAST, 0)
         for part, (lo, hi) in zip(gate_in, GATE_PARTS):
             nc.sync.dma_start(out=part[:], in_=gate[0, lo:hi].rearrange("(p i) -> p i", p=P))
-        load_x(ORDER[-1], 1)
-        for i in range(2):
-            nc.vector.memset(scales[i][:].bitcast(I32), 0)
+        load_x(LAST, 1)
+        for tile in scales:
+            nc.vector.memset(tile[:].bitcast(I32), 0)
         nc.vector.memset(codes[ORDER[0]][:, T:W], 0)
         nc.vector.memset(moved[:].bitcast(I32), 0)
         nc.vector.memset(ws[:].rearrange("p e n -> p (e n)").bitcast(I32), 0)
         load_weights(0)
 
         def interleave(a):
-            for lo, hi in QUANT[a]:
-                if (a, lo) == (ORDER[-1], QUANT[a][-1][0]):
-                    grouped[a, lo] = staged.tile([P, hi - lo, 4], BF16, name=f"grouped{a}_{lo}", offset=RAW_BYTES * PASSES, align_bytes=256)
+            for lo, hi in CHUNKS[a]:
+                if a == LAST and hi == T:
+                    grouped[a, lo] = staged.tile([P, hi - lo, 4], BF16, name=f"grouped{a}_{lo}", offset=CHUNK_AT, align_bytes=256)
                 else:
                     grouped[a, lo] = keep.tile([P, hi - lo, 4], BF16, name=f"grouped{a}_{lo}", align_bytes=256)
-            for engine, lo, hi in COPIES[a]:
-                first = max(l for l, h in QUANT[a] if l <= lo)
+
+            def views(chunk, lo, hi):
                 tile, start = [(t, l) for t, (l, h) in zip(raw[a], LOADS[a]) if l <= lo < h][0]
                 src = tile[:, :, lo - start : hi - start].rearrange("p t (c i) -> p c t i", i=4)
-                dest = grouped[a, first][:, lo - first : hi - first, :].rearrange("p (c i) t -> p c t i", i=4)
-                if engine == "scalar":
-                    nc.scalar.activation(dest, src, COPY)
-                else:
-                    nc.vector.tensor_copy(dest, src)
+                return grouped[a, chunk][:, lo - chunk : hi - chunk, :].rearrange("p (c i) t -> p c t i", i=4), src
+
+            begin, end = ON_SCALAR[a]
+            for lo, hi in sorted(CHUNKS[a]):
+                if max(lo, begin) < min(hi, end):
+                    nc.scalar.activation(*views(lo, max(lo, begin), min(hi, end)), COPY)
+            for lo, hi in CHUNKS[a]:
+                if hi <= begin or hi > end:
+                    nc.vector.tensor_copy(*views(lo, lo if hi <= begin else max(lo, end), hi))
 
         def quantize(a):
-            i, k = PLANE[a]
-            for lo, hi in QUANT[a]:
+            i, first = PLANE[a]
+            for lo, hi in CHUNKS[a]:
                 nc.vector.quantize_mx(
                     out=codes[a][:, lo:hi].bitcast(FP8X4),
-                    scales=scales[i][k:P, lo:hi],
+                    scales=scales[i][first:P, lo:hi],
                     in_=grouped[a, lo][:].rearrange("p w t -> p (w t)"),
                 )
 
-        def pick(dest, window, lo, hi):
-            cols = slice(C * lo, C * hi)
-            nc.vector.tensor_copy(dest[:, cols], window.indirect(offs_t[:, 8 * lo : 8 * hi]))
+        def gather(dest, window, lo, hi):
+            nc.vector.tensor_copy(dest, window.indirect(offs_t[:, LIST * lo : LIST * hi]))
 
-        def pick_codes(a, lo=0, hi=E):
-            pick(gcodes[a], codes[a].bitcast(U32), lo, hi)
-
-        def pick_late_codes(a, behind):
-            late[a] = staged.tile([P, C], U32, name=f"late{a}", offset=RAW_BYTES * behind + 11264, align_bytes=256)
-            nc.vector.tensor_copy(late[a][:], codes[a].bitcast(U32).indirect(offs_t[:, 8 * (E - 1) : 8 * E]))
-
-        def pick_scales(i):
-            pick(gscales[i], scales[i][:], 0, E)
-
-        def multiply(a, e, last_scales, tail_words):
-            i, k = PLANE[a]
+        def multiply(a, e, planes, tail_words):
+            i, first = PLANE[a]
             cols = slice(C * e, C * (e + 1))
             if a < PASSES8:
-                lhsT, lhsT_scale = w8[e][:, a, :].bitcast(FP8X4), ws[:, 2 * e + a, :]
+                lhsT, lhsT_scale = w8[e][:, a, :].bitcast(FP8X4), ws[:, PASSES8 * e + a, :]
             else:
-                lhsT, lhsT_scale = w4[e][:, a - 2, :].bitcast(FP4X4), ws[:, 2 * E + 3 * e + a - 2, :]
+                lhsT, lhsT_scale = w4[e][:, a - PASSES8, :].bitcast(FP4X4), ws[:, PASSES8 * E + PASSES4 * e + a - PASSES8, :]
             if a in tail_words:
                 words = tail_words[a][:]
             else:
                 words = late[a][:] if e == E - 1 else gcodes[a][:, cols]
+            if i == 1:
+                plane = planes[first:P, :]
+            else:
+                plane = moved[:, cols] if a == MOVED_PASS else gscales[first:P, cols]
             nc.tensor.matmul_mx(
                 out=acc[e][:, 0:C],
                 lhsT=lhsT,
                 lhsT_scale=lhsT_scale,
                 rhs=words.bitcast(FP8X4),
-                rhs_scale=last_scales[k:P, :] if i == 1 else moved[:, cols] if a == 3 else gscales[0][k:P, cols],
+                rhs_scale=plane,
                 start=(a == (SUM_ORDER if e else ORDER)[0]),
-                stop=(a == 4),
+                stop=(a == LAST),
             )
-
-        def place(e):
-            cols = slice(C * e, C * (e + 1))
-            nc.vector.tensor_tensor(y[:, cols], acc[e][:, 0:C], gate_t[:, cols], MULT)
-            nc.scalar.activation(placed[:].indirect(dst_t[:, 8 * e : 8 * (e + 1)]), y[:, cols], COPY)
 
         for before, a in zip([None] + ORDER, ORDER):
             interleave(a)
             quantize(a)
-            if before is not None and a != ORDER[-1]:
-                pick_late_codes(before, a)
-            if a not in ORDER[-2:]:
-                pick_codes(a, 0, E - 1)
-            if a == 3:
-                pick_scales(0)
-                nc.sync.dma_start(out=moved[0:112, :].bitcast(I32), in_=gscales[0][12:124, :].bitcast(I32))
-        for quad in range(4):
-            nc.sync.dma_start(out=ws[32 * quad : 32 * quad + 4, :, :].bitcast(I32), in_=ws_in[32 * quad : 32 * quad + 32 : 8, :, :].bitcast(I32))
-        for e in range(1, E):
+            if before is not None and a != LAST:
+                late[before] = staged.tile([P, C], U32, name=f"late{before}", offset=RAW_BYTES * a + LATE_AT, align_bytes=256)
+                gather(late[before][:], codes[before].bitcast(U32), E - 1, E)
+            if a in gcodes:
+                gather(gcodes[a][:, 0 : C * (E - 1)], codes[a].bitcast(U32), 0, E - 1)
+            if a == MOVED_PASS:
+                gather(gscales[:], scales[0][:], 0, E)
+                nc.sync.dma_start(out=moved[0:112, :].bitcast(I32), in_=gscales[12:124, :].bitcast(I32))
+        for q in range(4):
+            nc.sync.dma_start(out=ws[32 * q : 32 * q + 4, :, :].bitcast(I32), in_=ws_in[32 * q : 32 * q + 32 : 8, :, :].bitcast(I32))
+        load_weights(1)
+        nc.sync.dma_start(dst_t[:], dst)
+        for e in range(2, E):
             load_weights(e)
+
         make_identity(nc, ident[:])
-        gate_t = staged.tile([P, E * C], F32, name="gate_t", offset=RAW_BYTES * 4 + 9216, align_bytes=256)
+        gate_t = staged.tile([P, E * C], F32, name="gate_t", offset=GATE_AT, align_bytes=256)
         for part, bank, (lo, hi) in zip(gate_in, spread, GATE_PARTS):
             n = (hi - lo) // P
             for i in range(n):
                 nc.tensor.transpose(bank[:, P * i : P * (i + 1)], part[:, i : i + 1].to_broadcast([P, P]), ident[:])
             nc.scalar.activation(gate_t[:, lo:hi].rearrange("m (p i) -> m p i", i=n), bank[:, 0 : n * P].rearrange("m (i p) -> m p i", i=n), COPY)
 
-        def pick_ahead(e):
-            at = (RAW_BYTES * PASSES if e % 2 else RAW_BYTES * 4 + 8192 - 256) + 64 * (e // 2)
-            picked = offs_t[:, 8 * e : 8 * (e + 1)]
+        def gather_ahead(e):
+            at = (CHUNK_AT if e % 2 else SEAM - WORDS_BYTES // 2) + 64 * (e // 2)
             words = staged.tile([P, C], U32, name=f"fourth{e}", offset=at, align_bytes=64)
-            planes = staged.tile([P, C], U8, name=f"planes{e}", offset=at + 4 * C, align_bytes=64)
-            nc.vector.tensor_copy(planes[:], scales[1][:].indirect(picked))
-            nc.vector.tensor_copy(words[:], codes[1].bitcast(U32).indirect(picked))
+            planes = staged.tile([P, C], U8, name=f"planes{e}", offset=at + WORDS_BYTES, align_bytes=64)
+            gather(planes[:], scales[1][:], e, e + 1)
+            gather(words[:], codes[FOURTH].bitcast(U32), e, e + 1)
             return words, planes
 
-        def finish(e, fourth, planes):
-            last_words = staged.tile([P, C], U32, name=f"last{e}", offset=RAW_BYTES * PASSES + 2048 + LAST_AT[e], align_bytes=256)
-            nc.vector.tensor_copy(last_words[:], codes[4].bitcast(U32).indirect(offs_t[:, 8 * e : 8 * (e + 1)]))
+        def finish(e, fourth_words, planes):
+            last_words = staged.tile([P, C], U32, name=f"last{e}", offset=LAST_AT + LAST_HALVES[e] * WORDS_BYTES // 2, align_bytes=256)
+            gather(last_words[:], codes[LAST].bitcast(U32), e, e + 1)
             for a in SUM_ORDER if e else ORDER:
-                multiply(a, e, planes, {1: fourth, 4: last_words})
+                multiply(a, e, planes, {FOURTH: fourth_words, LAST: last_words})
 
-        finish(0, *pick_ahead(0))
-        ahead = pick_ahead(1)
+        def place(e):
+            cols = slice(C * e, C * (e + 1))
+            nc.vector.tensor_tensor(y[:, cols], acc[e][:, 0:C], gate_t[:, cols], MULT)
+            nc.scalar.activation(placed[:].indirect(dst_t[:, LIST * e : LIST * (e + 1)]), y[:, cols], COPY)
+
+        finish(0, *gather_ahead(0))
+        ahead = gather_ahead(1)
         place(0)
         finish(1, *ahead)
         for e in range(2, E - 1):
-            finish(e, *pick_ahead(e))
+            finish(e, *gather_ahead(e))
             place(e - 1)
-        ahead = pick_ahead(E - 1)
+        ahead = gather_ahead(E - 1)
         place(E - 2)
         finish(E - 1, *ahead)
         place(E - 1)

@@ -22,7 +22,7 @@ MULT = mybir.AluOpType.mult
 COPY = mybir.ActivationFunctionType.Copy
 
 ORDER = [2, 3, 0, 1, 4]
-FOURTH, LAST = ORDER[-2:]
+THIRD, FOURTH, LAST = ORDER[-3:]
 MOVED_PASS = 3
 PLANE = {2: (0, 0), 3: (0, 12), 0: (1, 4), 1: (1, 8), 4: (1, 0)}
 SUM_ORDER = [0, 2, 3, 1, 4]
@@ -44,9 +44,11 @@ WORDS_BYTES = 4 * C
 LATE_AT = RAW_BYTES - 2 * WORDS_BYTES
 SEAM = RAW_BYTES * LAST + 16 * LOADS[LAST][1][0]
 GATE_AT = SEAM + 2 * WORDS_BYTES
-CHUNK_AT = RAW_BYTES * PASSES
-LAST_AT = CHUNK_AT + 8 * 256
-LAST_HALVES = [1, 0, 2, 0, 2, 2]
+HALF = WORDS_BYTES // 2
+AREA_BYTES = C + 5 * HALF
+PLANES_AT = [RAW_BYTES * PASSES + AREA_BYTES * odd for odd in range(2)]
+WORDS_AT = [at + C + 2 * HALF for at in PLANES_AT]
+EARLY = {2: E - 1, 3: E - 1, 0: E - 1, 1: 1}
 
 
 def tile_moe_two_lin_none_kernel(tc, xT, w8_words, w8_scales, w4_words, w4_scales, gate, offs, dst, out):
@@ -70,12 +72,13 @@ def tile_moe_two_lin_none_kernel(tc, xT, w8_words, w8_scales, w4_words, w4_scale
         codes_all = keep.tile([P, (PASSES - 1) * T + W], I32, name="codes_all", align_bytes=256)
         codes = {a: codes_all[:, (PASSES - 1 - j) * T : (PASSES - 1 - j) * T + W] for j, a in enumerate(ORDER)}
         scales = [keep.tile([P, W], U8, name=f"scales{i}", align_bytes=256) for i in range(2)]
-        gcodes = {a: keep.tile([P, E * C], U32, name=f"gcodes{a}", align_bytes=256) for a in ORDER[:-2]}
+        gcodes = {a: keep.tile([P, n * C], U32, name=f"gcodes{a}", align_bytes=256) for a, n in EARLY.items()}
         gscales = keep.tile([P, E * C], U8, name="gscales0", align_bytes=256)
         moved = keep.tile([P, E * C], U8, name="moved", align_bytes=256)
         grouped = {}
         raw = {a: [staged.tile([P, 4, hi - lo], F32, name=f"raw{a}_{lo}", offset=RAW_BYTES * a + 16 * lo, align_bytes=256) for lo, hi in LOADS[a]] for a in range(PASSES)}
-        late = {}
+        words = {(a, e): gcodes[a][:, C * e : C * (e + 1)] for a, n in EARLY.items() for e in range(n)}
+        planes = {}
         acc = [psum.tile([N, 512], F32, name=f"acc{e}") for e in range(E)]
 
         w8_dram = w8_words.bitcast(I32).rearrange("e a p n u -> p (e a) (n u)")
@@ -94,11 +97,11 @@ def tile_moe_two_lin_none_kernel(tc, xT, w8_words, w8_scales, w4_words, w4_scale
 
         load_x(ORDER[0], 0)
         nc.sync.dma_start(offs_t[:], offs)
-        for a in ORDER[1:-1]:
+        for a in ORDER[1:]:
             load_x(a, 0)
         nc.sync.dma_start(out=ws_in[0:P:8, 0 : PASSES8 * E, :].bitcast(I32), in_=w8s_dram)
         nc.sync.dma_start(out=ws_in[0:P:8, PASSES8 * E :, :].bitcast(I32), in_=w4s_dram)
-        load_x(LAST, 0)
+        nc.sync.dma_start(dst_t[:], dst)
         for part, (lo, hi) in zip(gate_in, GATE_PARTS):
             nc.sync.dma_start(out=part[:], in_=gate[0, lo:hi].rearrange("(p i) -> p i", p=P))
         load_x(LAST, 1)
@@ -111,10 +114,7 @@ def tile_moe_two_lin_none_kernel(tc, xT, w8_words, w8_scales, w4_words, w4_scale
 
         def interleave(a):
             for lo, hi in CHUNKS[a]:
-                if a == LAST and hi == T:
-                    grouped[a, lo] = staged.tile([P, hi - lo, 4], BF16, name=f"grouped{a}_{lo}", offset=CHUNK_AT, align_bytes=256)
-                else:
-                    grouped[a, lo] = keep.tile([P, hi - lo, 4], BF16, name=f"grouped{a}_{lo}", align_bytes=256)
+                grouped[a, lo] = keep.tile([P, hi - lo, 4], BF16, name=f"grouped{a}_{lo}", align_bytes=256)
 
             def views(chunk, lo, hi):
                 tile, start = [(t, l) for t, (l, h) in zip(raw[a], LOADS[a]) if l <= lo < h][0]
@@ -141,26 +141,31 @@ def tile_moe_two_lin_none_kernel(tc, xT, w8_words, w8_scales, w4_words, w4_scale
         def gather(dest, window, lo, hi):
             nc.vector.tensor_copy(dest, window.indirect(offs_t[:, LIST * lo : LIST * hi]))
 
-        def multiply(a, e, planes, tail_words):
+        def gather_words(a, e, at):
+            tile = staged.tile([P, C], U32, name=f"words{a}_{e}", offset=at, align_bytes=64)
+            gather(tile[:], codes[a].bitcast(U32), e, e + 1)
+            words[a, e] = tile[:]
+
+        def gather_planes(e, at):
+            planes[e] = staged.tile([P, C], U8, name=f"planes{e}", offset=at, align_bytes=64)
+            gather(planes[e][:], scales[1][:], e, e + 1)
+
+        def multiply(a, e):
             i, first = PLANE[a]
             cols = slice(C * e, C * (e + 1))
             if a < PASSES8:
                 lhsT, lhsT_scale = w8[e][:, a, :].bitcast(FP8X4), ws[:, PASSES8 * e + a, :]
             else:
                 lhsT, lhsT_scale = w4[e][:, a - PASSES8, :].bitcast(FP4X4), ws[:, PASSES8 * E + PASSES4 * e + a - PASSES8, :]
-            if a in tail_words:
-                words = tail_words[a][:]
-            else:
-                words = late[a][:] if e == E - 1 else gcodes[a][:, cols]
             if i == 1:
-                plane = planes[first:P, :]
+                plane = planes[e][first:P, :]
             else:
                 plane = moved[:, cols] if a == MOVED_PASS else gscales[first:P, cols]
             nc.tensor.matmul_mx(
                 out=acc[e][:, 0:C],
                 lhsT=lhsT,
                 lhsT_scale=lhsT_scale,
-                rhs=words.bitcast(FP8X4),
+                rhs=words[a, e].bitcast(FP8X4),
                 rhs_scale=plane,
                 start=(a == (SUM_ORDER if e else ORDER)[0]),
                 stop=(a == LAST),
@@ -169,19 +174,16 @@ def tile_moe_two_lin_none_kernel(tc, xT, w8_words, w8_scales, w4_words, w4_scale
         for before, a in zip([None] + ORDER, ORDER):
             interleave(a)
             quantize(a)
-            if before is not None and a != LAST:
-                late[before] = staged.tile([P, C], U32, name=f"late{before}", offset=RAW_BYTES * a + LATE_AT, align_bytes=256)
-                gather(late[before][:], codes[before].bitcast(U32), E - 1, E)
+            if before in ORDER[:2]:
+                gather_words(before, E - 1, RAW_BYTES * a + LATE_AT)
             if a in gcodes:
-                gather(gcodes[a][:, 0 : C * (E - 1)], codes[a].bitcast(U32), 0, E - 1)
+                gather(gcodes[a][:], codes[a].bitcast(U32), 0, EARLY[a])
             if a == MOVED_PASS:
                 gather(gscales[:], scales[0][:], 0, E)
                 nc.sync.dma_start(out=moved[0:112, :].bitcast(I32), in_=gscales[12:124, :].bitcast(I32))
         for q in range(4):
             nc.sync.dma_start(out=ws[32 * q : 32 * q + 4, :, :].bitcast(I32), in_=ws_in[32 * q : 32 * q + 32 : 8, :, :].bitcast(I32))
-        load_weights(1)
-        nc.sync.dma_start(dst_t[:], dst)
-        for e in range(2, E):
+        for e in range(1, E):
             load_weights(e)
 
         make_identity(nc, ident[:])
@@ -192,34 +194,30 @@ def tile_moe_two_lin_none_kernel(tc, xT, w8_words, w8_scales, w4_words, w4_scale
                 nc.tensor.transpose(bank[:, P * i : P * (i + 1)], part[:, i : i + 1].to_broadcast([P, P]), ident[:])
             nc.scalar.activation(gate_t[:, lo:hi].rearrange("m (p i) -> m p i", i=n), bank[:, 0 : n * P].rearrange("m (i p) -> m p i", i=n), COPY)
 
-        def gather_ahead(e):
-            at = (CHUNK_AT if e % 2 else SEAM - WORDS_BYTES // 2) + 64 * (e // 2)
-            words = staged.tile([P, C], U32, name=f"fourth{e}", offset=at, align_bytes=64)
-            planes = staged.tile([P, C], U8, name=f"planes{e}", offset=at + WORDS_BYTES, align_bytes=64)
-            gather(planes[:], scales[1][:], e, e + 1)
-            gather(words[:], codes[FOURTH].bitcast(U32), e, e + 1)
-            return words, planes
-
-        def finish(e, fourth_words, planes):
-            last_words = staged.tile([P, C], U32, name=f"last{e}", offset=LAST_AT + LAST_HALVES[e] * WORDS_BYTES // 2, align_bytes=256)
-            gather(last_words[:], codes[LAST].bitcast(U32), e, e + 1)
+        def finish(e, at):
+            gather_words(LAST, e, at)
             for a in SUM_ORDER if e else ORDER:
-                multiply(a, e, planes, {FOURTH: fourth_words, LAST: last_words})
+                multiply(a, e)
 
         def place(e):
             cols = slice(C * e, C * (e + 1))
             nc.vector.tensor_tensor(y[:, cols], acc[e][:, 0:C], gate_t[:, cols], MULT)
             nc.scalar.activation(placed[:].indirect(dst_t[:, LIST * e : LIST * (e + 1)]), y[:, cols], COPY)
 
-        finish(0, *gather_ahead(0))
-        ahead = gather_ahead(1)
-        place(0)
-        finish(1, *ahead)
-        for e in range(2, E - 1):
-            finish(e, *gather_ahead(e))
-            place(e - 1)
-        ahead = gather_ahead(E - 1)
-        place(E - 2)
-        finish(E - 1, *ahead)
-        place(E - 1)
+        gather_words(FOURTH, 1, SEAM - HALF)
+        for e in range(E - 1):
+            at = WORDS_AT[e % 2] - HALF * (e // 2)
+            if e > 1:
+                gather_words(FOURTH, e, at + 2 * HALF)
+            gather_planes(e, PLANES_AT[e % 2])
+            finish(e, at)
+            if e > 0:
+                place(e - 1)
+        e = E - 1
+        gather_words(THIRD, e, WORDS_AT[e % 2] - HALF * (e // 2))
+        gather_words(FOURTH, e, WORDS_AT[e % 2] - HALF * (e // 2) + 2 * HALF)
+        gather_planes(e, PLANES_AT[e % 2])
+        place(e - 1)
+        finish(e, WORDS_AT[(e - 1) % 2] - HALF * ((e - 1) // 2))
+        place(e)
         nc.sync.dma_start(out=out, in_=placed[:])

@@ -19,36 +19,32 @@ U8 = mybir.dt.uint8
 FP8X4 = mybir.dt.float8_e4m3fn_x4
 FP4X4 = mybir.dt.float4_e2m1fn_x4
 MULT = mybir.AluOpType.mult
+ADD = mybir.AluOpType.add
 COPY = mybir.ActivationFunctionType.Copy
 
 ORDER = [2, 3, 0, 1, 4]
-THIRD, FOURTH, LAST = ORDER[-3:]
+LAST = ORDER[-1]
 MOVED_PASS = 3
 PLANE = {2: (0, 0), 3: (0, 12), 0: (1, 4), 1: (1, 8), 4: (1, 0)}
-SUM_ORDER = [0, 2, 3, 1, 4]
+HELD_ORDER = [0, 2, 3, 1, 4]
 LOADS = {a: [(0, 512), (512, T)] if a == LAST else [(0, T)] for a in range(PASSES)}
 CHUNKS = {
     2: [(512, T), (0, 256), (256, 512)],
     3: [(512, T), (0, 256), (256, 512)],
     0: [(0, 512), (512, T)],
     1: [(0, 256), (256, 512), (512, T)],
-    4: [(256, 512), (0, 256), (512, T)],
+    4: [(0, 256), (256, 512), (512, T)],
 }
-ON_SCALAR = {2: (0, 320), 3: (0, 384), 0: (0, 672), 1: (0, 608), 4: (256, T)}
+ON_SCALAR = {2: (0, 320), 3: (0, 384), 0: (0, 672), 1: (0, 576), 4: (0, T)}
 W = 1024
 LIST = C // 16
 GATE_PARTS = [(0, 512), (512, T)]
+STORES = [(0, T // 2), (T // 2, T)]
 
 RAW_BYTES = 4 * T * 4
 WORDS_BYTES = 4 * C
-LATE_AT = RAW_BYTES - 2 * WORDS_BYTES
-SEAM = RAW_BYTES * LAST + 16 * LOADS[LAST][1][0]
-GATE_AT = SEAM + 2 * WORDS_BYTES
-HALF = WORDS_BYTES // 2
-AREA_BYTES = C + 5 * HALF
-PLANES_AT = [RAW_BYTES * PASSES + AREA_BYTES * odd for odd in range(2)]
-WORDS_AT = [at + C + 2 * HALF for at in PLANES_AT]
-EARLY = {2: E - 1, 3: E - 1, 0: E - 1, 1: 1}
+LATE_AT = RAW_BYTES - WORDS_BYTES
+GATE_AT = RAW_BYTES * LAST + 16 * LOADS[LAST][1][0]
 
 
 def tile_moe_two_lin_none_kernel(tc, xT, w8_words, w8_scales, w4_words, w4_scales, gate, offs, dst, out):
@@ -56,7 +52,9 @@ def tile_moe_two_lin_none_kernel(tc, xT, w8_words, w8_scales, w4_words, w4_scale
     with ExitStack() as ctx:
         keep = ctx.enter_context(tc.tile_pool(name="keep", bufs=1))
         staged = ctx.enter_context(tc.tile_pool(name="staged", bufs=1))
+        ring = ctx.enter_context(tc.tile_pool(name="ring", bufs=2))
         psum = ctx.enter_context(tc.psum_pool(name="psum", bufs=1))
+        sums = ctx.enter_context(tc.psum_pool(name="sums", bufs=2))
 
         offs_t = keep.tile([P, T // 16], U16, name="offs_t")
         dst_t = keep.tile([P, T // 16], U16, name="dst_t")
@@ -68,18 +66,18 @@ def tile_moe_two_lin_none_kernel(tc, xT, w8_words, w8_scales, w4_words, w4_scale
         ident = keep.tile([P, P], F32, name="ident")
         spread = [psum.tile([P, 512], F32, name=f"spread{lo}") for lo, hi in GATE_PARTS]
         y = keep.tile([P, E * C], F32, name="y")
-        placed = keep.tile([P, T], F32, name="placed")
+        placed = [keep.tile([P, T], F32, name=f"placed{i}") for i in range(2)]
+        result = [keep.tile([P, hi - lo], F32, name=f"result{lo}") for lo, hi in STORES]
         codes_all = keep.tile([P, (PASSES - 1) * T + W], I32, name="codes_all", align_bytes=256)
         codes = {a: codes_all[:, (PASSES - 1 - j) * T : (PASSES - 1 - j) * T + W] for j, a in enumerate(ORDER)}
         scales = [keep.tile([P, W], U8, name=f"scales{i}", align_bytes=256) for i in range(2)]
-        gcodes = {a: keep.tile([P, n * C], U32, name=f"gcodes{a}", align_bytes=256) for a, n in EARLY.items()}
+        gcodes = {a: keep.tile([P, (E - 1) * C], U32, name=f"gcodes{a}", align_bytes=256) for a in ORDER[:-1]}
         gscales = keep.tile([P, E * C], U8, name="gscales0", align_bytes=256)
         moved = keep.tile([P, E * C], U8, name="moved", align_bytes=256)
         grouped = {}
         raw = {a: [staged.tile([P, 4, hi - lo], F32, name=f"raw{a}_{lo}", offset=RAW_BYTES * a + 16 * lo, align_bytes=256) for lo, hi in LOADS[a]] for a in range(PASSES)}
-        words = {(a, e): gcodes[a][:, C * e : C * (e + 1)] for a, n in EARLY.items() for e in range(n)}
-        planes = {}
-        acc = [psum.tile([N, 512], F32, name=f"acc{e}") for e in range(E)]
+        words = {(a, e): gcodes[a][:, C * e : C * (e + 1)] for a in gcodes for e in range(E - 1)}
+        acc = {}
 
         w8_dram = w8_words.bitcast(I32).rearrange("e a p n u -> p (e a) (n u)")
         w4_dram = w4_words.bitcast(I32).rearrange("e a p m -> p (e a) m")
@@ -110,6 +108,8 @@ def tile_moe_two_lin_none_kernel(tc, xT, w8_words, w8_scales, w4_words, w4_scale
         nc.vector.memset(codes[ORDER[0]][:, T:W], 0)
         nc.vector.memset(moved[:].bitcast(I32), 0)
         nc.vector.memset(ws[:].rearrange("p e n -> p (e n)").bitcast(I32), 0)
+        for window in placed:
+            nc.vector.memset(window[:], 0.0)
         load_weights(0)
 
         def interleave(a):
@@ -123,11 +123,14 @@ def tile_moe_two_lin_none_kernel(tc, xT, w8_words, w8_scales, w4_words, w4_scale
 
             begin, end = ON_SCALAR[a]
             for lo, hi in sorted(CHUNKS[a]):
-                if max(lo, begin) < min(hi, end):
-                    nc.scalar.activation(*views(lo, max(lo, begin), min(hi, end)), COPY)
+                nc_lo, nc_hi = max(lo, begin), min(hi, end)
+                if nc_lo < nc_hi:
+                    nc.scalar.activation(*views(lo, nc_lo, nc_hi), COPY)
             for lo, hi in CHUNKS[a]:
-                if hi <= begin or hi > end:
-                    nc.vector.tensor_copy(*views(lo, lo if hi <= begin else max(lo, end), hi))
+                if lo < begin:
+                    nc.vector.tensor_copy(*views(lo, lo, min(hi, begin)))
+                if hi > end:
+                    nc.vector.tensor_copy(*views(lo, max(lo, end), hi))
 
         def quantize(a):
             i, first = PLANE[a]
@@ -141,43 +144,15 @@ def tile_moe_two_lin_none_kernel(tc, xT, w8_words, w8_scales, w4_words, w4_scale
         def gather(dest, window, lo, hi):
             nc.vector.tensor_copy(dest, window.indirect(offs_t[:, LIST * lo : LIST * hi]))
 
-        def gather_words(a, e, at):
-            tile = staged.tile([P, C], U32, name=f"words{a}_{e}", offset=at, align_bytes=64)
-            gather(tile[:], codes[a].bitcast(U32), e, e + 1)
-            words[a, e] = tile[:]
-
-        def gather_planes(e, at):
-            planes[e] = staged.tile([P, C], U8, name=f"planes{e}", offset=at, align_bytes=64)
-            gather(planes[e][:], scales[1][:], e, e + 1)
-
-        def multiply(a, e):
-            i, first = PLANE[a]
-            cols = slice(C * e, C * (e + 1))
-            if a < PASSES8:
-                lhsT, lhsT_scale = w8[e][:, a, :].bitcast(FP8X4), ws[:, PASSES8 * e + a, :]
-            else:
-                lhsT, lhsT_scale = w4[e][:, a - PASSES8, :].bitcast(FP4X4), ws[:, PASSES8 * E + PASSES4 * e + a - PASSES8, :]
-            if i == 1:
-                plane = planes[e][first:P, :]
-            else:
-                plane = moved[:, cols] if a == MOVED_PASS else gscales[first:P, cols]
-            nc.tensor.matmul_mx(
-                out=acc[e][:, 0:C],
-                lhsT=lhsT,
-                lhsT_scale=lhsT_scale,
-                rhs=words[a, e].bitcast(FP8X4),
-                rhs_scale=plane,
-                start=(a == (SUM_ORDER if e else ORDER)[0]),
-                stop=(a == LAST),
-            )
-
         for before, a in zip([None] + ORDER, ORDER):
             interleave(a)
             quantize(a)
-            if before in ORDER[:2]:
-                gather_words(before, E - 1, RAW_BYTES * a + LATE_AT)
+            if before is not None:
+                late = staged.tile([P, C], U32, name=f"late{before}", offset=RAW_BYTES * a + LATE_AT, align_bytes=64)
+                gather(late[:], codes[before].bitcast(U32), E - 1, E)
+                words[before, E - 1] = late[:]
             if a in gcodes:
-                gather(gcodes[a][:], codes[a].bitcast(U32), 0, EARLY[a])
+                gather(gcodes[a][:], codes[a].bitcast(U32), 0, E - 1)
             if a == MOVED_PASS:
                 gather(gscales[:], scales[0][:], 0, E)
                 nc.sync.dma_start(out=moved[0:112, :].bitcast(I32), in_=gscales[12:124, :].bitcast(I32))
@@ -194,30 +169,49 @@ def tile_moe_two_lin_none_kernel(tc, xT, w8_words, w8_scales, w4_words, w4_scale
                 nc.tensor.transpose(bank[:, P * i : P * (i + 1)], part[:, i : i + 1].to_broadcast([P, P]), ident[:])
             nc.scalar.activation(gate_t[:, lo:hi].rearrange("m (p i) -> m p i", i=n), bank[:, 0 : n * P].rearrange("m (i p) -> m p i", i=n), COPY)
 
-        def finish(e, at):
-            gather_words(LAST, e, at)
-            for a in SUM_ORDER if e else ORDER:
-                multiply(a, e)
+        def finish(e):
+            cols = slice(C * e, C * (e + 1))
+            planes = ring.tile([P, C], U8, name="planes", align_bytes=64)
+            last_words = ring.tile([P, C], U32, name="last_words", align_bytes=64)
+            gather(planes[:], scales[1][:], e, e + 1)
+            gather(last_words[:], codes[LAST].bitcast(U32), e, e + 1)
+            words[LAST, e] = last_words[:]
+            acc[e] = sums.tile([N, 512], F32, name="acc")
+            order = HELD_ORDER if e == 1 else ORDER
+            for a in order:
+                i, first = PLANE[a]
+                if a < PASSES8:
+                    lhsT, lhsT_scale = w8[e][:, a, :].bitcast(FP8X4), ws[:, PASSES8 * e + a, :]
+                else:
+                    lhsT, lhsT_scale = w4[e][:, a - PASSES8, :].bitcast(FP4X4), ws[:, PASSES8 * E + PASSES4 * e + a - PASSES8, :]
+                if i == 1:
+                    plane = planes[first:P, :]
+                else:
+                    plane = moved[:, cols] if a == MOVED_PASS else gscales[first:P, cols]
+                nc.tensor.matmul_mx(
+                    out=acc[e][:, 0:C],
+                    lhsT=lhsT,
+                    lhsT_scale=lhsT_scale,
+                    rhs=words[a, e].bitcast(FP8X4),
+                    rhs_scale=plane,
+                    start=(a == order[0]),
+                    stop=(a == LAST),
+                )
 
         def place(e):
             cols = slice(C * e, C * (e + 1))
             nc.vector.tensor_tensor(y[:, cols], acc[e][:, 0:C], gate_t[:, cols], MULT)
-            nc.scalar.activation(placed[:].indirect(dst_t[:, LIST * e : LIST * (e + 1)]), y[:, cols], COPY)
+            window = placed[e % 2][:].indirect(dst_t[:, LIST * e : LIST * (e + 1)])
+            if e < E - 1:
+                nc.scalar.activation(window, y[:, cols], COPY)
+            else:
+                nc.vector.tensor_copy(window, y[:, cols])
 
-        gather_words(FOURTH, 1, SEAM - HALF)
-        for e in range(E - 1):
-            at = WORDS_AT[e % 2] - HALF * (e // 2)
-            if e > 1:
-                gather_words(FOURTH, e, at + 2 * HALF)
-            gather_planes(e, PLANES_AT[e % 2])
-            finish(e, at)
-            if e > 0:
-                place(e - 1)
-        e = E - 1
-        gather_words(THIRD, e, WORDS_AT[e % 2] - HALF * (e // 2))
-        gather_words(FOURTH, e, WORDS_AT[e % 2] - HALF * (e // 2) + 2 * HALF)
-        gather_planes(e, PLANES_AT[e % 2])
-        place(e - 1)
-        finish(e, WORDS_AT[(e - 1) % 2] - HALF * ((e - 1) // 2))
-        place(e)
-        nc.sync.dma_start(out=out, in_=placed[:])
+        finish(0)
+        for e in range(1, E):
+            finish(e)
+            place(e - 1)
+        place(E - 1)
+        for tile, (lo, hi) in zip(result, STORES):
+            nc.vector.tensor_tensor(tile[:], placed[0][:, lo:hi], placed[1][:, lo:hi], ADD)
+            nc.sync.dma_start(out=out[:, lo:hi], in_=tile[:])

@@ -33,9 +33,9 @@ CHUNKS = {
     3: [(512, T), (0, 256), (256, 512)],
     0: [(0, 512), (512, T)],
     1: [(0, 256), (256, 512), (512, T)],
-    4: [(0, 256), (256, 512), (512, T)],
+    4: [(256, 512), (0, 256), (512, T)],
 }
-ON_SCALAR = {2: (0, 320), 3: (0, 384), 0: (0, 672), 1: (0, 576), 4: (0, T)}
+ON_SCALAR = {2: (0, 320), 3: (0, 384), 0: (0, 672), 1: (0, 576), 4: (192, T)}
 W = 1024
 LIST = C // 16
 GATE_PARTS = [(0, 512), (512, T)]
@@ -114,7 +114,8 @@ def tile_moe_two_lin_none_kernel(tc, xT, w8_words, w8_scales, w4_words, w4_scale
 
         def interleave(a):
             for lo, hi in CHUNKS[a]:
-                grouped[a, lo] = keep.tile([P, hi - lo, 4], BF16, name=f"grouped{a}_{lo}", align_bytes=256)
+                shared = (a, lo) in [(ORDER[2], 512), (ORDER[3], 512), (LAST, 0)]
+                grouped[a, lo] = keep.tile([P, hi - lo, 4], BF16, name="grouped" if shared else f"grouped{a}_{lo}", align_bytes=256)
 
             def views(chunk, lo, hi):
                 tile, start = [(t, l) for t, (l, h) in zip(raw[a], LOADS[a]) if l <= lo < h][0]
@@ -122,14 +123,16 @@ def tile_moe_two_lin_none_kernel(tc, xT, w8_words, w8_scales, w4_words, w4_scale
                 return grouped[a, chunk][:, lo - chunk : hi - chunk, :].rearrange("p (c i) t -> p c t i", i=4), src
 
             begin, end = ON_SCALAR[a]
-            for lo, hi in sorted(CHUNKS[a]):
+            for lo, hi in sorted(CHUNKS[a]) if a != LAST else CHUNKS[a]:
                 nc_lo, nc_hi = max(lo, begin), min(hi, end)
                 if nc_lo < nc_hi:
                     nc.scalar.activation(*views(lo, nc_lo, nc_hi), COPY)
             for lo, hi in CHUNKS[a]:
                 if lo < begin:
-                    nc.vector.tensor_copy(*views(lo, lo, min(hi, begin)))
-                if hi > end:
+                    nc.gpsimd.tensor_copy(grouped[a, lo][:, 0:begin, :], raw[a][0][:, :, 0:begin].rearrange("p t w -> p w t"))
+                if hi > end and a == ORDER[3]:
+                    nc.gpsimd.tensor_copy(grouped[a, lo][:, end - lo :, :], raw[a][0][:, :, end:hi].rearrange("p t w -> p w t"))
+                elif hi > end:
                     nc.vector.tensor_copy(*views(lo, max(lo, end), hi))
 
         def quantize(a):

@@ -28,14 +28,9 @@ MOVED_PASS = 3
 PLANE = {2: (0, 0), 3: (0, 12), 0: (1, 4), 1: (1, 8), 4: (1, 0)}
 HELD_ORDER = [0, 2, 3, 1, 4]
 LOADS = {a: [(0, 512), (512, T)] if a == LAST else [(0, T)] for a in range(PASSES)}
-CHUNKS = {
-    2: [(512, T), (0, 256), (256, 512)],
-    3: [(512, T), (0, 256), (256, 512)],
-    0: [(0, 512), (512, T)],
-    1: [(0, 256), (256, 512), (512, T)],
-    4: [(256, 512), (0, 256), (512, T)],
-}
-ON_SCALAR = {2: (0, 320), 3: (0, 384), 0: (0, 672), 1: (0, 576), 4: (192, T)}
+CHUNKS = {a: [(512, T), (0, 256), (256, 512)] for a in range(PASSES)}
+CHUNKS[LAST] = [(0, 256), (256, 512), (512, T)]
+ON_SCALAR = {ORDER[0]: 320, ORDER[1]: 384}
 W = 1024
 LIST = C // 16
 GATE_PARTS = [(0, 512), (512, T)]
@@ -89,8 +84,10 @@ def tile_moe_two_lin_none_kernel(tc, xT, w8_words, w8_scales, w4_words, w4_scale
             lo, hi = LOADS[a][part]
             nc.sync.dma_start(out=raw[a][part][:], in_=rows[:, :, lo:hi])
 
-        def load_weights(e):
+        def load_w4(e):
             nc.sync.dma_start(out=w4[e][:].bitcast(I32), in_=w4_dram[:, PASSES4 * e : PASSES4 * (e + 1), :])
+
+        def load_w8(e):
             nc.sync.dma_start(out=w8[e][:].bitcast(I32), in_=w8_dram[:, PASSES8 * e : PASSES8 * (e + 1), :])
 
         load_x(ORDER[0], 0)
@@ -99,7 +96,6 @@ def tile_moe_two_lin_none_kernel(tc, xT, w8_words, w8_scales, w4_words, w4_scale
             load_x(a, 0)
         nc.sync.dma_start(out=ws_in[0:P:8, 0 : PASSES8 * E, :].bitcast(I32), in_=w8s_dram)
         nc.sync.dma_start(out=ws_in[0:P:8, PASSES8 * E :, :].bitcast(I32), in_=w4s_dram)
-        nc.sync.dma_start(dst_t[:], dst)
         for part, (lo, hi) in zip(gate_in, GATE_PARTS):
             nc.sync.dma_start(out=part[:], in_=gate[0, lo:hi].rearrange("(p i) -> p i", p=P))
         load_x(LAST, 1)
@@ -110,30 +106,32 @@ def tile_moe_two_lin_none_kernel(tc, xT, w8_words, w8_scales, w4_words, w4_scale
         nc.vector.memset(ws[:].rearrange("p e n -> p (e n)").bitcast(I32), 0)
         for window in placed:
             nc.vector.memset(window[:], 0.0)
-        load_weights(0)
+        load_w4(0)
+        for r in range(4):
+            nc.sync.dma_start(out=ws[r:P:32, :, :].bitcast(I32), in_=ws_in[8 * r : P : 32, :, :].bitcast(I32))
 
-        def interleave(a):
-            for lo, hi in CHUNKS[a]:
-                shared = (a, lo) in [(ORDER[2], 512), (ORDER[3], 512), (LAST, 0)]
-                grouped[a, lo] = keep.tile([P, hi - lo, 4], BF16, name="grouped" if shared else f"grouped{a}_{lo}", align_bytes=256)
+        def interleave(before, a):
+            names = [f"edge{before}" if a not in ON_SCALAR else f"first{a}", f"middle{a}", f"edge{a}"]
+            for (lo, hi), name in zip(CHUNKS[a], names):
+                grouped[a, lo] = keep.tile([P, hi - lo, 4], BF16, name=name, align_bytes=256)
+
+            def source(lo, hi):
+                tile, start = [(t, l) for t, (l, h) in zip(raw[a], LOADS[a]) if l <= lo < h][0]
+                return tile[:, :, lo - start : hi - start]
 
             def views(chunk, lo, hi):
-                tile, start = [(t, l) for t, (l, h) in zip(raw[a], LOADS[a]) if l <= lo < h][0]
-                src = tile[:, :, lo - start : hi - start].rearrange("p t (c i) -> p c t i", i=4)
+                src = source(lo, hi).rearrange("p t (c i) -> p c t i", i=4)
                 return grouped[a, chunk][:, lo - chunk : hi - chunk, :].rearrange("p (c i) t -> p c t i", i=4), src
 
-            begin, end = ON_SCALAR[a]
-            for lo, hi in sorted(CHUNKS[a]) if a != LAST else CHUNKS[a]:
-                nc_lo, nc_hi = max(lo, begin), min(hi, end)
-                if nc_lo < nc_hi:
-                    nc.scalar.activation(*views(lo, nc_lo, nc_hi), COPY)
-            for lo, hi in CHUNKS[a]:
-                if lo < begin:
-                    nc.gpsimd.tensor_copy(grouped[a, lo][:, 0:begin, :], raw[a][0][:, :, 0:begin].rearrange("p t w -> p w t"))
-                if hi > end and a == ORDER[3]:
-                    nc.gpsimd.tensor_copy(grouped[a, lo][:, end - lo :, :], raw[a][0][:, :, end:hi].rearrange("p t w -> p w t"))
-                elif hi > end:
-                    nc.vector.tensor_copy(*views(lo, max(lo, end), hi))
+            first, middle, last = CHUNKS[a]
+            split = ON_SCALAR.get(a, last[1])
+            nc.scalar.activation(*views(middle[0], *middle), COPY)
+            nc.scalar.activation(*views(last[0], last[0], split), COPY)
+            if a in ON_SCALAR:
+                nc.vector.tensor_copy(*views(first[0], *first))
+                nc.vector.tensor_copy(*views(last[0], split, last[1]))
+            else:
+                nc.gpsimd.tensor_copy(grouped[a, first[0]][:], source(*first).rearrange("p t w -> p w t"))
 
         def quantize(a):
             i, first = PLANE[a]
@@ -148,7 +146,7 @@ def tile_moe_two_lin_none_kernel(tc, xT, w8_words, w8_scales, w4_words, w4_scale
             nc.vector.tensor_copy(dest, window.indirect(offs_t[:, LIST * lo : LIST * hi]))
 
         for before, a in zip([None] + ORDER, ORDER):
-            interleave(a)
+            interleave(before, a)
             quantize(a)
             if before is not None:
                 late = staged.tile([P, C], U32, name=f"late{before}", offset=RAW_BYTES * a + LATE_AT, align_bytes=64)
@@ -159,10 +157,13 @@ def tile_moe_two_lin_none_kernel(tc, xT, w8_words, w8_scales, w4_words, w4_scale
             if a == MOVED_PASS:
                 gather(gscales[:], scales[0][:], 0, E)
                 nc.sync.dma_start(out=moved[0:112, :].bitcast(I32), in_=gscales[12:124, :].bitcast(I32))
-        for q in range(4):
-            nc.sync.dma_start(out=ws[32 * q : 32 * q + 4, :, :].bitcast(I32), in_=ws_in[32 * q : 32 * q + 32 : 8, :, :].bitcast(I32))
-        for e in range(1, E):
-            load_weights(e)
+        load_w8(0)
+        load_w8(1)
+        load_w4(1)
+        nc.sync.dma_start(dst_t[:], dst)
+        for e in range(2, E):
+            load_w4(e)
+            load_w8(e)
 
         make_identity(nc, ident[:])
         gate_t = staged.tile([P, E * C], F32, name="gate_t", offset=GATE_AT, align_bytes=256)

@@ -28,13 +28,17 @@ MOVED_PASS = 3
 PLANE = {2: (0, 0), 3: (0, 12), 0: (1, 4), 1: (1, 8), 4: (1, 0)}
 HELD_ORDER = [0, 2, 3, 1, 4]
 LOADS = {a: [(0, 512), (512, T)] if a == LAST else [(0, T)] for a in range(PASSES)}
-CHUNKS = {a: [(512, T), (0, 256), (256, 512)] for a in range(PASSES)}
-CHUNKS[LAST] = [(0, 256), (256, 512), (512, T)]
-ON_SCALAR = {ORDER[0]: 320, ORDER[1]: 384}
+CHUNKS = {
+    2: [[("vector", 512, T)], [("scalar", 0, 256)], [("scalar", 256, 320), ("vector", 320, 512)]],
+    3: [[("vector", 512, T)], [("scalar", 0, 256)], [("scalar", 256, 384), ("vector", 384, 512)]],
+    0: [[("gpsimd", 512, T)], [("scalar", 0, 256)], [("scalar", 256, 512)]],
+    1: [[("gpsimd", 512, T)], [("scalar", 0, 256)], [("scalar", 256, 512)]],
+    4: [[("gpsimd", 0, 256)], [("scalar", 256, 512)], [("scalar", 512, T)]],
+}
 W = 1024
 LIST = C // 16
 GATE_PARTS = [(0, 512), (512, T)]
-STORES = [(0, T // 2), (T // 2, T)]
+STORES = [(0, 256), (256, 512), (512, T)]
 
 RAW_BYTES = 4 * T * 4
 WORDS_BYTES = 4 * C
@@ -96,9 +100,9 @@ def tile_moe_two_lin_none_kernel(tc, xT, w8_words, w8_scales, w4_words, w4_scale
             load_x(a, 0)
         nc.sync.dma_start(out=ws_in[0:P:8, 0 : PASSES8 * E, :].bitcast(I32), in_=w8s_dram)
         nc.sync.dma_start(out=ws_in[0:P:8, PASSES8 * E :, :].bitcast(I32), in_=w4s_dram)
+        load_x(LAST, 1)
         for part, (lo, hi) in zip(gate_in, GATE_PARTS):
             nc.sync.dma_start(out=part[:], in_=gate[0, lo:hi].rearrange("(p i) -> p i", p=P))
-        load_x(LAST, 1)
         for tile in scales:
             nc.vector.memset(tile[:].bitcast(I32), 0)
         nc.vector.memset(codes[ORDER[0]][:, T:W], 0)
@@ -111,36 +115,32 @@ def tile_moe_two_lin_none_kernel(tc, xT, w8_words, w8_scales, w4_words, w4_scale
             nc.sync.dma_start(out=ws[r:P:32, :, :].bitcast(I32), in_=ws_in[8 * r : P : 32, :, :].bitcast(I32))
 
         def interleave(before, a):
-            names = [f"edge{before}" if a not in ON_SCALAR else f"first{a}", f"middle{a}", f"edge{a}"]
-            for (lo, hi), name in zip(CHUNKS[a], names):
-                grouped[a, lo] = keep.tile([P, hi - lo, 4], BF16, name=name, align_bytes=256)
-
-            def source(lo, hi):
-                tile, start = [(t, l) for t, (l, h) in zip(raw[a], LOADS[a]) if l <= lo < h][0]
-                return tile[:, :, lo - start : hi - start]
-
-            def views(chunk, lo, hi):
-                src = source(lo, hi).rearrange("p t (c i) -> p c t i", i=4)
-                return grouped[a, chunk][:, lo - chunk : hi - chunk, :].rearrange("p (c i) t -> p c t i", i=4), src
-
-            first, middle, last = CHUNKS[a]
-            split = ON_SCALAR.get(a, last[1])
-            nc.scalar.activation(*views(middle[0], *middle), COPY)
-            nc.scalar.activation(*views(last[0], last[0], split), COPY)
-            if a in ON_SCALAR:
-                nc.vector.tensor_copy(*views(first[0], *first))
-                nc.vector.tensor_copy(*views(last[0], split, last[1]))
-            else:
-                nc.gpsimd.tensor_copy(grouped[a, first[0]][:], source(*first).rearrange("p t w -> p w t"))
+            for j, parts in enumerate(CHUNKS[a]):
+                name = f"edge{before}" if parts[0][0] == "gpsimd" else f"first{a}" if j == 0 else f"edge{a}" if j == len(CHUNKS[a]) - 1 else f"middle{a}"
+                first, end = parts[0][1], parts[-1][2]
+                tile = keep.tile([P, end - first, 4], BF16, name=name, align_bytes=256)
+                grouped[a, first, end] = tile
+                for engine, lo, hi in parts:
+                    loaded, start = [(t, l) for t, (l, h) in zip(raw[a], LOADS[a]) if l <= lo < h][0]
+                    dest, src = tile[:, lo - first : hi - first, :], loaded[:, :, lo - start : hi - start]
+                    if engine == "gpsimd":
+                        nc.gpsimd.tensor_copy(dest, src.rearrange("p t w -> p w t"))
+                        continue
+                    dest, src = dest.rearrange("p (c i) t -> p c t i", i=4), src.rearrange("p t (c i) -> p c t i", i=4)
+                    if engine == "scalar":
+                        nc.scalar.activation(dest, src, COPY)
+                    else:
+                        nc.vector.tensor_copy(dest, src)
 
         def quantize(a):
             i, first = PLANE[a]
-            for lo, hi in CHUNKS[a]:
-                nc.vector.quantize_mx(
-                    out=codes[a][:, lo:hi].bitcast(FP8X4),
-                    scales=scales[i][first:P, lo:hi],
-                    in_=grouped[a, lo][:].rearrange("p w t -> p (w t)"),
-                )
+            for (b, lo, hi), tile in grouped.items():
+                if b == a:
+                    nc.vector.quantize_mx(
+                        out=codes[a][:, lo:hi].bitcast(FP8X4),
+                        scales=scales[i][first:P, lo:hi],
+                        in_=tile[:].rearrange("p w t -> p (w t)"),
+                    )
 
         def gather(dest, window, lo, hi):
             nc.vector.tensor_copy(dest, window.indirect(offs_t[:, LIST * lo : LIST * hi]))

@@ -33,7 +33,7 @@ CHUNKS = {
     3: [[("vector", 512, T)], [("scalar", 0, 256)], [("scalar", 256, 384), ("vector", 384, 512)]],
     0: [[("gpsimd", 512, T)], [("scalar", 0, 256)], [("scalar", 256, 512)]],
     1: [[("gpsimd", 512, T)], [("scalar", 0, 256)], [("scalar", 256, 512)]],
-    4: [[("gpsimd", 0, 256)], [("scalar", 256, 512)], [("scalar", 512, T)]],
+    4: [[("gpsimd", 0, 224), ("scalar", 224, 256)], [("scalar", 256, 512)], [("scalar", 512, T)]],
 }
 W = 1024
 LIST = C // 16
@@ -117,7 +117,7 @@ def tile_moe_two_lin_none_kernel(tc, xT, w8_words, w8_scales, w4_words, w4_scale
         def interleave(before, a):
             for j, parts in enumerate(CHUNKS[a]):
                 name = f"edge{before}" if parts[0][0] == "gpsimd" else f"first{a}" if j == 0 else f"edge{a}" if j == len(CHUNKS[a]) - 1 else f"middle{a}"
-                first, end = parts[0][1], parts[-1][2]
+                first, end = min(lo for engine, lo, hi in parts), max(hi for engine, lo, hi in parts)
                 tile = keep.tile([P, end - first, 4], BF16, name=name, align_bytes=256)
                 grouped[a, first, end] = tile
                 for engine, lo, hi in parts:
@@ -126,7 +126,8 @@ def tile_moe_two_lin_none_kernel(tc, xT, w8_words, w8_scales, w4_words, w4_scale
                     if engine == "gpsimd":
                         nc.gpsimd.tensor_copy(dest, src.rearrange("p t w -> p w t"))
                         continue
-                    dest, src = dest.rearrange("p (c i) t -> p c t i", i=4), src.rearrange("p t (c i) -> p c t i", i=4)
+                    n = 2 if engine == "scalar" else 4
+                    dest, src = dest.rearrange("p (c i) t -> p c t i", i=n), src.rearrange("p t (c i) -> p c t i", i=n)
                     if engine == "scalar":
                         nc.scalar.activation(dest, src, COPY)
                     else:

@@ -26,6 +26,7 @@ ORDER = [2, 3, 0, 1, 4]
 LAST = ORDER[-1]
 MOVED_PASS = 3
 PLANE = {2: (0, 0), 3: (0, 12), 0: (1, 4), 1: (1, 8), 4: (1, 0)}
+BEHIND = 2
 HELD_ORDER = [0, 2, 3, 1, 4]
 LOADS = {a: [(0, 512), (512, T)] if a == LAST else [(0, T)] for a in range(PASSES)}
 CHUNKS = {
@@ -38,6 +39,7 @@ CHUNKS = {
 W = 1024
 LIST = C // 16
 GATE_PARTS = [(0, 512), (512, T)]
+SCATTERS = [(0, 128), (128, 256), (256, 384), (384, 480), (480, 640), (640, T)]
 STORES = [(0, 256), (256, 512), (512, T)]
 
 RAW_BYTES = 4 * T * 4
@@ -51,9 +53,9 @@ def tile_moe_two_lin_none_kernel(tc, xT, w8_words, w8_scales, w4_words, w4_scale
     with ExitStack() as ctx:
         keep = ctx.enter_context(tc.tile_pool(name="keep", bufs=1))
         staged = ctx.enter_context(tc.tile_pool(name="staged", bufs=1))
-        ring = ctx.enter_context(tc.tile_pool(name="ring", bufs=2))
+        ring = ctx.enter_context(tc.tile_pool(name="ring", bufs=BEHIND + 1))
         psum = ctx.enter_context(tc.psum_pool(name="psum", bufs=1))
-        sums = ctx.enter_context(tc.psum_pool(name="sums", bufs=2))
+        sums = ctx.enter_context(tc.psum_pool(name="sums", bufs=BEHIND + 1))
 
         offs_t = keep.tile([P, T // 16], U16, name="offs_t")
         dst_t = keep.tile([P, T // 16], U16, name="dst_t")
@@ -159,10 +161,11 @@ def tile_moe_two_lin_none_kernel(tc, xT, w8_words, w8_scales, w4_words, w4_scale
                 gather(gscales[:], scales[0][:], 0, E)
                 nc.sync.dma_start(out=moved[0:112, :].bitcast(I32), in_=gscales[12:124, :].bitcast(I32))
         load_w8(0)
-        load_w8(1)
-        load_w4(1)
+        for e in range(1, BEHIND + 1):
+            load_w8(e)
+            load_w4(e)
         nc.sync.dma_start(dst_t[:], dst)
-        for e in range(2, E):
+        for e in range(BEHIND + 1, E):
             load_w4(e)
             load_w8(e)
 
@@ -182,7 +185,7 @@ def tile_moe_two_lin_none_kernel(tc, xT, w8_words, w8_scales, w4_words, w4_scale
             gather(last_words[:], codes[LAST].bitcast(U32), e, e + 1)
             words[LAST, e] = last_words[:]
             acc[e] = sums.tile([N, 512], F32, name="acc")
-            order = HELD_ORDER if e == 1 else ORDER
+            order = HELD_ORDER if 0 < e <= BEHIND else ORDER
             for a in order:
                 i, first = PLANE[a]
                 if a < PASSES8:
@@ -206,17 +209,18 @@ def tile_moe_two_lin_none_kernel(tc, xT, w8_words, w8_scales, w4_words, w4_scale
         def place(e):
             cols = slice(C * e, C * (e + 1))
             nc.vector.tensor_tensor(y[:, cols], acc[e][:, 0:C], gate_t[:, cols], MULT)
-            window = placed[e % 2][:].indirect(dst_t[:, LIST * e : LIST * (e + 1)])
+            lo, hi = SCATTERS[e]
+            window = placed[e % 2][:].indirect(dst_t[:, lo // 16 : hi // 16])
             if e < E - 1:
-                nc.scalar.activation(window, y[:, cols], COPY)
+                nc.scalar.activation(window, y[:, lo:hi], COPY)
             else:
-                nc.vector.tensor_copy(window, y[:, cols])
+                nc.vector.tensor_copy(window, y[:, lo:hi])
 
-        finish(0)
-        for e in range(1, E):
-            finish(e)
-            place(e - 1)
-        place(E - 1)
+        for e in range(E + BEHIND):
+            if e < E:
+                finish(e)
+            if e >= BEHIND:
+                place(e - BEHIND)
         for tile, (lo, hi) in zip(result, STORES):
             nc.vector.tensor_tensor(tile[:], placed[0][:, lo:hi], placed[1][:, lo:hi], ADD)
             nc.sync.dma_start(out=out[:, lo:hi], in_=tile[:])

from contextlib import ExitStack

import concourse.mybir as mybir
from concourse.masks import make_identity

K, T, E, C, N = 2560, 768, 6, 128, 128
P = 128
PASSES = 5
PASSES8 = 2
PASSES4 = PASSES - PASSES8
FLOPS = 2 * K * N * E * C

F32 = mybir.dt.float32
BF16 = mybir.dt.bfloat16
I32 = mybir.dt.int32
U32 = mybir.dt.uint32
U16 = mybir.dt.uint16
U8 = mybir.dt.uint8
FP8X4 = mybir.dt.float8_e4m3fn_x4
FP4X4 = mybir.dt.float4_e2m1fn_x4
MULT = mybir.AluOpType.mult
ADD = mybir.AluOpType.add
COPY = mybir.ActivationFunctionType.Copy

ORDER = [2, 3, 0, 1, 4]
LAST = ORDER[-1]
MOVED_PASS = 3
PLANE = {2: (0, 0), 3: (0, 12), 0: (1, 4), 1: (1, 8), 4: (1, 0)}
BEHIND = 2
HELD_ORDER = [0, 2, 3, 1, 4]
LOADS = {a: [(0, 512), (512, T)] if a == LAST else [(0, T)] for a in range(PASSES)}
CHUNKS = {
    2: [[("vector", 512, T)], [("scalar", 0, 256)], [("scalar", 256, 320), ("vector", 320, 512)]],
    3: [[("vector", 512, T)], [("scalar", 0, 256)], [("scalar", 256, 384), ("vector", 384, 512)]],
    0: [[("gpsimd", 512, T)], [("scalar", 0, 256)], [("scalar", 256, 512)]],
    1: [[("gpsimd", 512, T)], [("scalar", 0, 256)], [("scalar", 256, 512)]],
    4: [[("gpsimd", 0, 224), ("scalar", 224, 256)], [("scalar", 256, 512)], [("scalar", 512, T)]],
}
W = 1024
LIST = C // 16
GATE_PARTS = [(0, 512), (512, T)]
SCATTERS = [(0, 128), (128, 256), (256, 384), (384, 480), (480, 640), (640, T)]
STORES = [(0, 256), (256, 512), (512, T)]

RAW_BYTES = 4 * T * 4
WORDS_BYTES = 4 * C
LATE_AT = RAW_BYTES - WORDS_BYTES
GATE_AT = RAW_BYTES * LAST + 16 * LOADS[LAST][1][0]


def tile_moe_two_lin_none_kernel(tc, xT, w8_words, w8_scales, w4_words, w4_scales, gate, offs, dst, out):
    nc = tc.nc
    with ExitStack() as ctx:
        keep = ctx.enter_context(tc.tile_pool(name="keep", bufs=1))
        staged = ctx.enter_context(tc.tile_pool(name="staged", bufs=1))
        ring = ctx.enter_context(tc.tile_pool(name="ring", bufs=BEHIND + 1))
        psum = ctx.enter_context(tc.psum_pool(name="psum", bufs=1))
        sums = ctx.enter_context(tc.psum_pool(name="sums", bufs=BEHIND + 1))

        offs_t = keep.tile([P, T // 16], U16, name="offs_t")
        dst_t = keep.tile([P, T // 16], U16, name="dst_t")
        w8 = [keep.tile([P, PASSES8, 4 * N], U8, name=f"w8_{e}", align_bytes=256) for e in range(E)]
        w4 = [keep.tile([P, PASSES4, 2 * N], U8, name=f"w4_{e}", align_bytes=256) for e in range(E)]
        gate_in = [keep.tile([P, (hi - lo) // P], F32, name=f"gate_in{lo}") for lo, hi in GATE_PARTS]
        ws = keep.tile([P, E * PASSES, N], U8, name="ws", align_bytes=256)
        ws_in = keep.tile([P, E * PASSES, N], U8, name="ws_in", align_bytes=256)
        ident = keep.tile([P, P], F32, name="ident")
        spread = [psum.tile([P, 512], F32, name=f"spread{lo}") for lo, hi in GATE_PARTS]
        y = keep.tile([P, E * C], F32, name="y")
        placed = [keep.tile([P, T], F32, name=f"placed{i}") for i in range(2)]
        result = [keep.tile([P, hi - lo], F32, name=f"result{lo}") for lo, hi in STORES]
        codes_all = keep.tile([P, (PASSES - 1) * T + W], I32, name="codes_all", align_bytes=256)
        codes = {a: codes_all[:, (PASSES - 1 - j) * T : (PASSES - 1 - j) * T + W] for j, a in enumerate(ORDER)}
        scales = [keep.tile([P, W], U8, name=f"scales{i}", align_bytes=256) for i in range(2)]
        gcodes = {a: keep.tile([P, (E - 1) * C], U32, name=f"gcodes{a}", align_bytes=256) for a in ORDER[:-1]}
        gscales = keep.tile([P, E * C], U8, name="gscales0", align_bytes=256)
        moved = keep.tile([P, E * C], U8, name="moved", align_bytes=256)
        grouped = {}
        raw = {a: [staged.tile([P, 4, hi - lo], F32, name=f"raw{a}_{lo}", offset=RAW_BYTES * a + 16 * lo, align_bytes=256) for lo, hi in LOADS[a]] for a in range(PASSES)}
        words = {(a, e): gcodes[a][:, C * e : C * (e + 1)] for a in gcodes for e in range(E - 1)}
        acc = {}

        w8_dram = w8_words.bitcast(I32).rearrange("e a p n u -> p (e a) (n u)")
        w4_dram = w4_words.bitcast(I32).rearrange("e a p m -> p (e a) m")
        w8s_dram = w8_scales.bitcast(I32).rearrange("e a q n -> q (e a) n")
        w4s_dram = w4_scales.bitcast(I32).rearrange("e a q n -> q (e a) n")

        def load_x(a, part):
            rows = xT[512 * a : 512 * (a + 1), :].rearrange("(p t) w -> p t w", t=4)
            lo, hi = LOADS[a][part]
            nc.sync.dma_start(out=raw[a][part][:], in_=rows[:, :, lo:hi])

        def load_w4(e):
            nc.sync.dma_start(out=w4[e][:].bitcast(I32), in_=w4_dram[:, PASSES4 * e : PASSES4 * (e + 1), :])

        def load_w8(e):
            nc.sync.dma_start(out=w8[e][:].bitcast(I32), in_=w8_dram[:, PASSES8 * e : PASSES8 * (e + 1), :])

        load_x(ORDER[0], 0)
        nc.sync.dma_start(offs_t[:], offs)
        for a in ORDER[1:]:
            load_x(a, 0)
        nc.sync.dma_start(out=ws_in[0:P:8, 0 : PASSES8 * E, :].bitcast(I32), in_=w8s_dram)
        nc.sync.dma_start(out=ws_in[0:P:8, PASSES8 * E :, :].bitcast(I32), in_=w4s_dram)
        load_x(LAST, 1)
        for part, (lo, hi) in zip(gate_in, GATE_PARTS):
            nc.sync.dma_start(out=part[:], in_=gate[0, lo:hi].rearrange("(p i) -> p i", p=P))
        for tile in scales:
            nc.vector.memset(tile[:].bitcast(I32), 0)
        nc.vector.memset(codes[ORDER[0]][:, T:W], 0)
        nc.vector.memset(moved[:].bitcast(I32), 0)
        nc.vector.memset(ws[:].rearrange("p e n -> p (e n)").bitcast(I32), 0)
        for window in placed:
            nc.vector.memset(window[:], 0.0)
        load_w4(0)
        for r in range(4):
            nc.sync.dma_start(out=ws[r:P:32, :, :].bitcast(I32), in_=ws_in[8 * r : P : 32, :, :].bitcast(I32))

        def interleave(before, a):
            for j, parts in enumerate(CHUNKS[a]):
                name = f"edge{before}" if parts[0][0] == "gpsimd" else f"first{a}" if j == 0 else f"edge{a}" if j == len(CHUNKS[a]) - 1 else f"middle{a}"
                first, end = min(lo for engine, lo, hi in parts), max(hi for engine, lo, hi in parts)
                tile = keep.tile([P, end - first, 4], BF16, name=name, align_bytes=256)
                grouped[a, first, end] = tile
                for engine, lo, hi in parts:
                    loaded, start = [(t, l) for t, (l, h) in zip(raw[a], LOADS[a]) if l <= lo < h][0]
                    dest, src = tile[:, lo - first : hi - first, :], loaded[:, :, lo - start : hi - start]
                    if engine == "gpsimd":
                        nc.gpsimd.tensor_copy(dest, src.rearrange("p t w -> p w t"))
                        continue
                    n = 2 if engine == "scalar" else 4
                    dest, src = dest.rearrange("p (c i) t -> p c t i", i=n), src.rearrange("p t (c i) -> p c t i", i=n)
                    if engine == "scalar":
                        nc.scalar.activation(dest, src, COPY)
                    else:
                        nc.vector.tensor_copy(dest, src)

        def quantize(a):
            i, first = PLANE[a]
            for (b, lo, hi), tile in grouped.items():
                if b == a:
                    nc.vector.quantize_mx(
                        out=codes[a][:, lo:hi].bitcast(FP8X4),
                        scales=scales[i][first:P, lo:hi],
                        in_=tile[:].rearrange("p w t -> p (w t)"),
                    )

        def gather(dest, window, lo, hi):
            nc.vector.tensor_copy(dest, window.indirect(offs_t[:, LIST * lo : LIST * hi]))

        for before, a in zip([None] + ORDER, ORDER):
            interleave(before, a)
            quantize(a)
            if before is not None:
                late = staged.tile([P, C], U32, name=f"late{before}", offset=RAW_BYTES * a + LATE_AT, align_bytes=64)
                gather(late[:], codes[before].bitcast(U32), E - 1, E)
                words[before, E - 1] = late[:]
            if a in gcodes:
                gather(gcodes[a][:], codes[a].bitcast(U32), 0, E - 1)
            if a == MOVED_PASS:
                gather(gscales[:], scales[0][:], 0, E)
                nc.sync.dma_start(out=moved[0:112, :].bitcast(I32), in_=gscales[12:124, :].bitcast(I32))
        load_w8(0)
        for e in range(1, BEHIND + 1):
            load_w8(e)
            load_w4(e)
        nc.sync.dma_start(dst_t[:], dst)
        for e in range(BEHIND + 1, E):
            load_w4(e)
            load_w8(e)

        make_identity(nc, ident[:])
        gate_t = staged.tile([P, E * C], F32, name="gate_t", offset=GATE_AT, align_bytes=256)
        for part, bank, (lo, hi) in zip(gate_in, spread, GATE_PARTS):
            n = (hi - lo) // P
            for i in range(n):
                nc.tensor.transpose(bank[:, P * i : P * (i + 1)], part[:, i : i + 1].to_broadcast([P, P]), ident[:])
            nc.scalar.activation(gate_t[:, lo:hi].rearrange("m (p i) -> m p i", i=n), bank[:, 0 : n * P].rearrange("m (i p) -> m p i", i=n), COPY)

        def finish(e):
            cols = slice(C * e, C * (e + 1))
            planes = ring.tile([P, C], U8, name="planes", align_bytes=64)
            last_words = ring.tile([P, C], U32, name="last_words", align_bytes=64)
            gather(planes[:], scales[1][:], e, e + 1)
            gather(last_words[:], codes[LAST].bitcast(U32), e, e + 1)
            words[LAST, e] = last_words[:]
            acc[e] = sums.tile([N, 512], F32, name="acc")
            order = HELD_ORDER if 0 < e <= BEHIND else ORDER
            for a in order:
                i, first = PLANE[a]
                if a < PASSES8:
                    lhsT, lhsT_scale = w8[e][:, a, :].bitcast(FP8X4), ws[:, PASSES8 * e + a, :]
                else:
                    lhsT, lhsT_scale = w4[e][:, a - PASSES8, :].bitcast(FP4X4), ws[:, PASSES8 * E + PASSES4 * e + a - PASSES8, :]
                if i == 1:
                    plane = planes[first:P, :]
                else:
                    plane = moved[:, cols] if a == MOVED_PASS else gscales[first:P, cols]
                nc.tensor.matmul_mx(
                    out=acc[e][:, 0:C],
                    lhsT=lhsT,
                    lhsT_scale=lhsT_scale,
                    rhs=words[a, e].bitcast(FP8X4),
                    rhs_scale=plane,
                    start=(a == order[0]),
                    stop=(a == LAST),
                )

        def place(e):
            cols = slice(C * e, C * (e + 1))
            nc.vector.tensor_tensor(y[:, cols], acc[e][:, 0:C], gate_t[:, cols], MULT)
            lo, hi = SCATTERS[e]
            window = placed[e % 2][:].indirect(dst_t[:, lo // 16 : hi // 16])
            if e < E - 1:
                nc.scalar.activation(window, y[:, lo:hi], COPY)
            else:
                nc.vector.tensor_copy(window, y[:, lo:hi])

        for e in range(E + BEHIND):
            if e < E:
                finish(e)
            if e >= BEHIND:
                place(e - BEHIND)
        for tile, (lo, hi) in zip(result, STORES):
            nc.vector.tensor_tensor(tile[:], placed[0][:, lo:hi], placed[1][:, lo:hi], ADD)
            nc.sync.dma_start(out=out[:, lo:hi], in_=tile[:])
